import numpy as np, ml_dtypes
CORES = [10,34,74,98]
N = 4
import mx_ref
BF = ml_dtypes.bfloat16
def gcols(t, e):
    v = np.concatenate([t.reshape(8, 16, -1, 4), np.zeros((8, 16, 1, 4), BF)], axis=2)
    return np.ascontiguousarray(np.stack([v[g][:, e[g]] for g in range(8)])).reshape(128, -1)
def tile(rs):
    return np.stack(rs, axis=2).reshape(128, -1).astype(BF)
def cut(t, i, w=512):
    return t[:, w * i:w * i + w]
def pick(q, e):
    c = np.concatenate([q[0].reshape(128, -1, 4), np.zeros((128, 1, 4), np.uint8)], axis=1); s = np.concatenate([q[1], np.ones((16, 1), np.uint8)], axis=1)
    return (np.ascontiguousarray(c[:, e].reshape(128, -1)), np.ascontiguousarray(s[:, e]))
def join(*qs):
    return (np.concatenate([q[0] for q in qs], axis=1), np.concatenate([q[1] for q in qs], axis=1))
def put(q, e, v):
    c, s = q[0].reshape(128, -1, 4).copy(), q[1].copy(); c[:, e] = v[0].reshape(128, -1, 4); s[:, e] = v[1]
    return (c.reshape(128, -1), s)
def pk(c, s):
    return (np.ascontiguousarray(c), mx_ref.live(s))
def emit(q):
    return q[0], q[1]
def packed(v, rng):
    q = [mx_ref.quantize(np.ascontiguousarray(v[r])) for r in range(N)]
    return np.stack([a for a, b in q]), np.stack([mx_ref.plane(b, rng) for a, b in q])
def values_of_codes():
    e, c = np.zeros((128, 128, 4), np.float32), np.zeros((128, 2, 4), np.uint8)
    e[np.arange(128), np.arange(128), 0] = 1
    c[:127, :, 0] = np.arange(256).reshape(2, 128).T[:127]
    return mx_ref.matmul(mx_ref.quantize(e.reshape(128, 512).astype(BF)), (c.reshape(128, 8), np.full((16, 2), 127, np.uint8))).T.reshape(-1).astype(np.float64)
CODE_VALUE, SCALE_VALUE = values_of_codes(), 2.0 ** (np.arange(256) - 127.0)
def decode(q):
    return (CODE_VALUE[q[0]].reshape(16, 8, -1, 4) * SCALE_VALUE[q[1]][:, None, :, None] + 0.0).reshape(128, -1).astype(np.float32)
def f(rng, *shape):
    return mx_ref.flush((rng.standard_normal(shape, dtype=np.float32) * np.exp2(rng.integers(-2, 3, shape[:-1] + (1,)))).astype(BF))
def wide(rng, *shape, cols=0):
    v = rng.standard_normal(shape, dtype=np.float32) * np.exp2(rng.integers(-12, 13, shape)).astype(np.float32)
    if cols: v *= np.repeat(np.exp2(rng.integers(-cols, cols + 1, shape[:-2] + (1, shape[-1] // 4))) * (rng.random(shape[:-2] + (1, shape[-1] // 4)) > 0.0625), 4, axis=-1).astype(np.float32)
    return mx_ref.flush(v.astype(BF))
C, B, F, K, R = 384, 9, 3, 3, 2
T = 2 ** B
def keys(p):
    m = (p.reshape(8, 16, C) < 0).astype(np.int64)
    return np.sum(m[:, :B] << np.arange(B)[:, None], axis=1), np.sum(m[:, B:B + F] << np.arange(F)[:, None], axis=1)
def insert(a):
    slots, free = np.full((8, T), -1), np.ones((8, C), bool)
    for k in range(K):
        for g in range(8):
            s = (a[g] + k) % T
            want = np.flatnonzero(free[g] & (slots[g][s] < 0))
            at, first = np.unique(s[want], return_index=True)
            slots[g, at] = want[first]
            free[g, want[first]] = False
    return slots
def search(slots, held, a, h):
    found = np.full((8, C), -1)
    for k in range(K):
        c = np.take_along_axis(slots, (a + k) % T, axis=1)
        hit = (found < 0) & (c >= 0) & (np.take_along_axis(held, np.maximum(c, 0), axis=1) == h)
        found[hit] = c[hit]
    return found
def numbers_of(rng):
    return {"x": np.array(f(rng, N, 128, 4 * C)), "u": np.array(f(rng, N, 128, 512)), "v": np.array(f(rng, N, 128, 512))}
def weights(rng, w):
    c, p = packed(w, rng)
    return {"wc": c, "ws": p}
def still(rng):
    w = np.zeros((N, 128, 4, 128, 4), np.float32)
    i = np.arange(128)
    for b in range(4): w[:, i, b, i, b] = 32
    return weights(rng, w.reshape(N, 128, 2048).astype(BF))
def spots(rng):
    e = np.stack([np.concatenate([[0, T - 1], 1 + rng.permutation(T - 2)[:C - 2]]) for g in range(8)])
    return rng.permuted(np.tile(e, (N, 1, 1)), axis=2)
def plant(d, rng, a, h, size, look):
    x, u = d["x"].reshape(N, 8, 16, C, 4), d["u"].reshape(N, 128, 8, 16, 4)
    k = ((a + (h << B))[..., None] >> np.arange(16)) & 1
    m = np.where(k == 1, -1.0, rng.integers(0, 2, k.shape)) * size[:, None, None, None]
    m[..., B + F:] = 0
    x[:, :, :8] = 0
    x[:, :, :4] = m.reshape(N, 8, C, 4, 4).transpose(0, 1, 3, 2, 4).astype(np.float32).astype(BF)
    u[:, :, :, :B + F] = 0
    for g in range(8):
        for i in range(B + F): u[:, 16 * g + i // 4, g, i, i % 4] = look.astype(np.float32).astype(BF)
    return {"x": x.reshape(N, 128, 4 * C), "u": u.reshape(N, 128, 512), "v": d["v"], **still(rng)}
def setup_inputs(rng):
    return {**numbers_of(rng), **weights(rng, f(rng, N, 128, 2048))}
def setup_inputs_crowd(rng):
    s = T - C // 4 - 4
    a = (s + np.repeat(np.arange(C // 2), np.tile([3, 1, 0, 4, 0, 0, 6, 2], C // 16))) % T
    a = rng.permuted(np.tile(a, (N, 8, 1)), axis=2)
    e = int(rng.integers(N))
    o = rng.permutation(8)
    m = np.where(o % 2 == 0, C // 32, rng.integers(0, C // 16, 8))
    z = (s + 3 + 8 * ((m + 1 + rng.integers(0, C // 16 - 1, 8)) % (C // 16))) % T
    a[e] = ((s + 3 + 8 * m) % T)[:, None]
    h = rng.integers(0, 2 ** F, (N, 8, C))
    b, n = (e - 1) % N, (e + 1) % N
    for g in range(8):
        if o[g] < 4:
            a[e, g, C - K:] = z[g]
            h[e, g, C - K:] = rng.permutation(2 ** F)[:K]
            j = np.flatnonzero(a[b, g] == z[g])[0]
            a[b, g, j] = a[b, g, C - 1]
            a[b, g, C - 1] = z[g]
            h[b, g, a[b, g] == z[g]] = h[e, g, C - 1]
        else:
            h[e, g, K:] = h[n, g, np.flatnonzero(a[n, g] == a[e, g, 0])[0]]
    size = np.where((np.arange(N) + rng.integers(2)) % 2 == 0, 64.0, 1.0)
    return plant(numbers_of(rng), rng, a, h, size, np.ones(N))
def setup_inputs_found(rng):
    e = int(rng.integers(N))
    a = spots(rng)
    z, c = (e + 2) % N, int(rng.integers(1, C))
    for g in range(8):
        a[z, g, np.flatnonzero(a[z, g] == 0)[0]] = a[z, g, c]
        a[z, g, c] = 0
    h = np.tile(rng.integers(0, 2 ** F, (8, 1)) * (rng.permutation(8) % 2)[:, None], (N, 1, C))
    h[e] = (h[e] + 1) % 2 ** F
    d = plant(numbers_of(rng), rng, a, h, np.ones(N), np.ones(N))
    x = d["x"].reshape(N, 128, C, 4)
    x[z, :, c] = 0
    return {**d, "x": x.reshape(N, 128, 4 * C)}
def setup_inputs_sizes(rng):
    small = (np.arange(N) + rng.integers(N)) % N < N // 2
    a = spots(rng)
    h = rng.integers(0, 2 ** F, (N, 8, C))
    return plant(numbers_of(rng), rng, a, h, np.where(small, 2.0 ** -30, 2.0 ** 27), np.where(small, 2.0 ** -30, 2.0 ** 30))
def setup_inputs_spread(rng):
    d = setup_inputs(rng)
    d["x"] = wide(rng, N, 128, 4 * C, cols=6)
    return d
def check_inputs(d):
    b = []
    for k in ("x", "u", "v"):
        a = np.abs(d[k].astype(np.float32))
        if not (np.isfinite(a).all() and ((a == 0) | (a >= 2.0 ** -30) & (a <= 2.0 ** 30)).all()): b.append("a value of " + k)
    c, s = d["wc"] & 127, np.stack([mx_ref.live(p) for p in d["ws"]])
    if (c == 127).any(): b.append("a code of wc")
    if ((s < 85) | (s > 160))[c.reshape(N, 16, 8, 512, 4).max(axis=(2, 4)) > 0].any(): b.append("a scale of ws")
    return b
def reference(x, u, v, wc, ws):
    qu = [mx_ref.quantize(u[r]) for r in range(N)]
    lay = [pk(wc[r], ws[r]) for r in range(N)]
    now = [x[r] for r in range(N)]
    for t in range(R):
        made, a, h, slots, answers = [], [], [], [], []
        for r in range(N):
            q = mx_ref.quantize(now[r])
            made.append(tile([mx_ref.matmul(pick(lay[r], np.arange(128 * b, 128 * b + 128)), q) * np.float32(0.03125) for b in range(4)]))
            mx_ref.quantize(made[r])
            i, j = keys(mx_ref.matmul(qu[r], q))
            a.append(i)
            h.append(j)
            slots.append(insert(i))
        for r in range(N):
            n = (r + 1) % N
            answers.append(mx_ref.quantize(gcols(made[n], search(slots[n], h[n], a[r], h[r]))))
        came = decode(join(*answers))
        now = [(made[r].astype(np.float32) + cut(came, r, 4 * C)).astype(BF) for r in range(N)]
    y = np.zeros((N, 128, C), np.float32)
    oc, osc = np.zeros((N, 128, 4 * C), np.uint8), np.zeros((N, 16, C), np.uint8)
    for r in range(N):
        q = mx_ref.quantize(now[r])
        y[r] = mx_ref.matmul(mx_ref.quantize(v[r]), q)
        oc[r], osc[r] = emit(q)
    return {"y": y, "oc": oc, "osc": osc}

@@ -1,0 +1,472 @@
+from concourse.mybir import dt, AluOpType as A, ActivationFunctionType as F
+
+C = 384
+ROUNDS = 2
+H16 = "float16"
+HUGE = 8388608.0
+X4 = "float8_e4m3fn_x4"
+SPANS = ((0, 256), (256, C))
+
+
+def sb(n, dtype):
+    return ("sbuf", [128, n], dtype)
+
+
+SCRATCH = {
+    "ps": ("psum", [128, 4096], "float32"),
+    "ut": sb(512, "bfloat16"), "vt": sb(512, "bfloat16"), "uq": sb(128, X4), "us": sb(128, "uint8"),
+    "vq": sb(128, X4), "vs": sb(128, "uint8"), "wq": sb(512, X4), "wp": sb(512, "uint8"),
+    "fm": sb(2048, "bfloat16"), "fq": sb(512, X4), "fs": sb(512, "uint8"),
+    "em": sb(2560, "bfloat16"), "eq": sb(640, X4), "es": sb(640, "uint8"),
+    "pint": sb(8, "int32"), "tint": sb(12, "int32"), "col": sb(24, "float32"),
+    "krow": sb(64, "float32"), "eqm": sb(64, "float32"), "mul": sb(64, "float32"), "pw": sb(64, "float32"),
+    "vrow": sb(64, "float32"), "vb": sb(64, "int32"), "vc": sb(64, "int32"), "sg": sb(64, "bfloat16"),
+    "qrow": sb(128, "bfloat16"), "grow": sb(128, "bfloat16"), "wmask": sb(128, "bfloat16"),
+    "ones": sb(128, "bfloat16"), "ident": sb(128, "bfloat16"),
+    "j8": sb(C, "float32"), "wcon": sb(C, "float32"), "k16": sb(C, "bfloat16"), "diag": sb(C, "bfloat16"),
+    "r32": sb(832, "bfloat16"), "r16": sb(C, "bfloat16"), "k512": sb(288, "bfloat16"),
+    "crow": sb(64, "float32"), "row16": sb(8, "float32"), "lp": sb(2, "uint16"), "lq": sb(2, "uint16"), "lsh": sb(8, "uint16"),
+    "bits": sb(4 * C, "bfloat16"), "bq": sb(C, X4), "bs": sb(C, "uint8"),
+    "a0": sb(416, "bfloat16"), "a1": sb(416, "bfloat16"), "b0": sb(416, H16), "b1": sb(416, H16),
+    "cum": sb(832, H16), "base": sb(2, "float32"), "junk": sb(C, "bfloat16"),
+    "key": sb(C, "float32"), "srt": sb(C, "float32"), "zt": sb(832, H16), "zs": sb(832, H16),
+    "zw": sb(96, "float32"), "zu": sb(64, "float32"), "lpos": sb(32, "uint16"),
+    "ymin": sb(3 * 392, "float32"), "firsts": sb(224, "float32"), "ta": sb(288, "float32"), "tb": sb(128, "float32"),
+    "r1": sb(34, "float32"), "r2": sb(34, "float32"), "r3": sb(34, "float32"), "r4": sb(34, "float32"),
+    "vi": sb(34, "int32"), "vf": sb(34, "int32"), "vn": sb(34, "int32"), "vg": sb(34, "float32"),
+    "hsg": sb(C, "bfloat16"), "him": sb(C, "bfloat16"), "dg": sb(C, H16), "dgs": sb(C, H16), "lask": sb(24, "uint16"),
+    "dist": sb(288, "float32"), "ans": sb(288, "float32"),
+    "z2": sb(C, H16), "zt2": sb(C, H16), "zs2": sb(C, H16), "fi": sb(24, "int32"), "fj": sb(96, "int32"), "fu": sb(64, "int32"),
+    "lfound": sb(32, "uint16"), "dwin": sb(4 * 392, "float32"), "yb": sb(C, "float32"),
+}
+for _t in range(ROUNDS + 1):
+    SCRATCH["x%d" % _t] = sb(4 * C, "bfloat16")
+    SCRATCH["xq%d" % _t] = sb(C, X4)
+    SCRATCH["xs%d" % _t] = sb(C, "uint8")
+for _t in range(ROUNDS):
+    SCRATCH["p%d" % _t] = sb(4 * C, "bfloat16")
+    SCRATCH["pq%d" % _t] = sb(C, X4)
+    SCRATCH["pp%d" % _t] = sb(C, "uint8")
+    SCRATCH["nq%d" % _t] = sb(C, X4)
+    SCRATCH["np%d" % _t] = sb(C, "uint8")
+    SCRATCH["tab%d" % _t] = sb(34, "float32")
+    SCRATCH["land%d" % _t] = sb(34, "float32")
+
+NPOOL = 120
+SEMAPHORES = ["s%d" % _i for _i in range(NPOOL)] + ["sent"] + ["gotp%d" % _t for _t in range(ROUNDS)] + ["gott%d" % _t for _t in range(ROUNDS)]
+
+CI, CL, CG, CGI, CQ, CB2, CB3, C31, CB, CM1, CW, CNL, CF, CSH, CO, CE, C64, CH, CA, CA8 = range(20)
+PS, PSH, PL, PW, PH = 15, 24, 36, 43, 59
+
+
+def meet(r, s):
+    if r[0] != s[0]:
+        return False
+    if r[0] == "ps":
+        return r[1] // 512 <= (s[2] - 1) // 512 and s[1] // 512 <= (r[2] - 1) // 512
+    if r[2] <= s[1] or s[2] <= r[1]:
+        return False
+    return not (r[3] == s[3] and r[3] > 1 and (r[1] - s[1]) % r[3])
+
+
+def emit(g, T, ops):
+    queues = {"g": g, "v": g.vector, "a": g.scalar, "t": g.tensor, "s": g.sync}
+    known = {k: set() for k in queues}
+    before, waits, needed = [], [], set()
+    for i, (q, kind, fn, rd, wr) in enumerate(ops):
+        deps = []
+        for j in range(i - 1, -1, -1):
+            if j in known[q]:
+                continue
+            q2, kind2, _, rd2, wr2 = ops[j]
+            hit = any(meet(r, s) for r in rd + wr for s in wr2) or any(meet(r, s) for r in wr for s in rd2)
+            if not hit and q2 != q:
+                hit = any(r[0] == "ps" and meet(r, s) for r in rd for s in rd2)
+            if hit:
+                deps.append(j)
+                known[q] = known[q] | before[j] | {j}
+        waits.append(deps)
+        needed.update(deps)
+        before.append(set() if kind == "arrive" else known[q])
+    last, mark = [], {}
+    for i, (q, kind, fn, rd, wr) in enumerate(ops):
+        if kind == "arrive":
+            mark[i] = fn
+            continue
+        for j in reversed(waits[i]):
+            queues[q].wait_ge(T.sem[mark[j][0]], mark[j][1])
+        call = fn()
+        if i in needed:
+            k = len(last)
+            if kind == "op":
+                for n in range(len(last)):
+                    if last[n][2] == "op" and last[n][0] in before[i]:
+                        k = n
+                        break
+            if k == len(last):
+                last.append((i, 0, kind))
+            step = 1 if kind == "op" else 16
+            last[k] = (i, last[k][1] + step, kind)
+            mark[i] = ("s%d" % k, last[k][1])
+            call.then_inc(T.sem["s%d" % k], step)
+
+
+def rank_program(g, core, T, topo):
+    rank = T.rank_of(core)
+    if rank is None:
+        return
+    n = len(T.cores)
+    to = T.cores[(rank - 1) % n]
+    frm = T.cores[(rank + 1) % n]
+    rid, pid, _ = topo.addr(to)
+    mask = topo.mask(core, to)
+    lanes_out, lanes_in = len(topo.engines(core, to)), len(topo.engines(frm, core))
+    ops = []
+    V, S, PE = g.vector, g.scalar, g.tensor
+
+    def R(name, lo=0, hi=None, step=1):
+        return (name, lo, SCRATCH[name][1][1] if hi is None else hi, step)
+
+    def col(k):
+        return R("col", k, k + 1)
+
+    def pw(k):
+        return R("pw", k, k + 1)
+
+    def bank(k, w=C):
+        return R("ps", 512 * k, 512 * k + w)
+
+    def ap(r):
+        if not isinstance(r, tuple):
+            return r
+        if len(r) == 2:
+            return ap(r[0]).indirect(ap(r[1]))
+        return T[r[0]][:, r[1]:r[2]:r[3]] if r[3] > 1 else T[r[0]][:, r[1]:r[2]]
+
+    def runs(*rs):
+        out = []
+        for r in rs:
+            if isinstance(r, tuple):
+                out += list(r) if len(r) == 2 else [r]
+        return out
+
+    def add(q, fn, rd, wr, kind="op"):
+        ops.append((q, kind, fn, rd, wr))
+
+    def memset(o, c):
+        add("v", lambda: V.memset(ap(o), c), [], [o])
+
+    def copy(o, i):
+        if len(o) == 2:
+            add("v", lambda: V.tensor_copy(ap(o), ap(i)), runs(i, o[1]), [o[0]])
+        else:
+            add("v", lambda: V.tensor_copy(ap(o), ap(i)), runs(i), [o])
+
+    def ts(o, i, s1, op0, s2=None, op1=None):
+        if op1 is None:
+            add("v", lambda: V.tensor_scalar(ap(o), ap(i), ap(s1), None, op0), runs(i, s1), [o])
+        else:
+            add("v", lambda: V.tensor_scalar(ap(o), ap(i), ap(s1), ap(s2), op0, op1), runs(i, s1, s2), [o])
+
+    def tt(o, i0, i1, op):
+        add("v", lambda: V.tensor_tensor(ap(o), ap(i0), ap(i1), op), runs(i0, i1), [o])
+
+    def scan(o, d0, d1, init, op0, op1):
+        add("v", lambda: V.tensor_tensor_scan(ap(o), ap(d0), ap(d1), ap(init), op0, op1), runs(d0, d1, init), [o])
+
+    def turn(o, i):
+        add("v", lambda: V.transpose(ap(o), ap(i)), [i], [o])
+
+    def quant(c, s, i, lo=0, hi=None):
+        hi = SCRATCH[c][1][1] if hi is None else hi
+        a, b, d = R(c, lo, hi), R(s, lo, hi), R(i, 4 * lo, 4 * hi)
+        add("v", lambda: V.quantize_mx(ap(a), ap(b), ap(d)), [d], [a, b])
+
+    def act(o, i, func, bias=None, scale=None, acc=None):
+        kw = {}
+        if bias is not None:
+            kw["bias"] = bias
+        if scale is not None:
+            kw["scale"] = scale
+        if acc is not None:
+            kw["accum_out"] = acc
+        add("a", lambda: S.activation(ap(o), ap(i), func, **{k: ap(w) for k, w in kw.items()}), runs(i, bias, scale), runs(o, acc))
+
+    def fill(o, c):
+        act(o, R("r32", 0, len(range(o[1], o[2], o[3]))), F.Identity, bias=c, scale=0.0)
+
+    def mm(k, lq, ls, at, rq, rs, lo=0, hi=C):
+        o = bank(k, hi - lo)
+        four = [R(lq, 128 * at, 128 * at + 128), R(ls, 128 * at, 128 * at + 128), R(rq, lo, hi), R(rs, lo, hi)]
+        add("t", lambda: PE.matmul_mx(ap(o), *[ap(r) for r in four], True, True), four, [o])
+
+    def iota(o, pattern, base, mult):
+        if SCRATCH[o[0]][2] == "int32":
+            add("g", lambda: g.iota(ap(o), pattern, base, mult), [], [o])
+        else:
+            add("g", lambda: g.iota(ap(o), pattern, base, mult, allow_small_or_imprecise_dtypes=True), [], [o])
+
+    def dma(q, out, in_, rd, wr):
+        eng = {"a": S, "s": g.sync}[q]
+        add(q, lambda: eng.dma_start(out(), in_()), rd, wr, "dma")
+
+    def send(dst, src, sem, codes=False):
+        def call():
+            o, i = ap(R(dst)), ap(R(src))
+            if codes:
+                o, i = o.bitcast(dt.uint8), i.bitcast(dt.uint8)
+            return g.remote_dma(o, i, T.sem[sem], T.sem.sent, pid, rid, mask)
+        add("g", call, [R(src)], [], "send")
+
+    def arrive(sem, count, bufs):
+        add("g", (sem, count), [], [R(b) for b in bufs], "arrive")
+
+    for lo, hi in SPANS:
+        dma("s", lambda lo=lo, hi=hi: T.x0[:, 4 * lo:4 * hi], lambda lo=lo, hi=hi: T.x[:, 4 * lo:4 * hi], [], [R("x0", 4 * lo, 4 * hi)])
+    dma("a", lambda: T.ut[:], lambda: T.u[:], [], [R("ut")])
+    dma("s", lambda: T.wp[:], lambda: T.ws[:], [], [R("wp")])
+    for lo in (0, 256):
+        dma("s", lambda lo=lo: T.wq[:, lo:lo + 256].bitcast(dt.uint8), lambda lo=lo: T.wc[:, 4 * lo:4 * lo + 1024], [], [R("wq", lo, lo + 256)])
+    dma("s", lambda: T.vt[:], lambda: T.v[:], [], [R("vt")])
+    for t in range(ROUNDS):
+        arrive("gotp%d" % t, 2 * lanes_in, ["nq%d" % t, "np%d" % t])
+        arrive("gott%d" % t, lanes_in, ["land%d" % t])
+
+    iota(R("pint", 0, 1), [[0, 1]], 0, 1)
+    iota(R("krow", 0, 16), [[-1, 16]], 15, 0)
+    iota(R("krow", 16, 64), [[0, 3], [1, 16]], 0, 0)
+    iota(R("vrow", 0, 32), [[-1, 32]], 31, 0)
+    iota(R("vrow", 32, 64), [[0, 2], [32, 16]], 0, 0)
+    iota(R("qrow"), [[1, 4], [0, 32]], 0, 0)
+    iota(R("grow"), [[1, 8], [0, 16]], 0, 0)
+    iota(R("j8"), [[8, C]], 0, 0)
+    iota(R("pint", 2, 4), [[0, 2]], 0, 17)
+    iota(R("pint", 4, 5), [[0, 1]], 15, 1)
+    iota(R("row16"), [[64, 4], [16, 2]], 0, 0)
+    iota(R("crow", 0, 32), [[-16384, 32]], 16384 * 31, 0)
+    iota(R("crow", 32, 64), [[-16384, 32]], 16384 * 31 - 8192, 0)
+    iota(R("k16"), [[0, 24], [1, 16]], 0, 0)
+    memset(R("fm", 0, 1024), 0.0)
+    act(R("fm", 1024, 2048), R("fm", 0, 1024), F.Copy)
+    act(R("bits", 0, 1024), R("fm", 1024, 2048), F.Copy)
+    memset(R("mul", 0, 32), 2.0)
+    memset(R("mul", 32, 64), 1.0)
+    p0 = R("pint", 0, 1)
+    ts(R("tint", CI, CI + 1), p0, 15, A.bitwise_and)
+    ts(R("tint", CL, CL + 1), p0, 31, A.bitwise_and)
+    ts(R("tint", CG, CG + 1), p0, 4, A.logical_shift_right, 1, A.bitwise_and)
+    ts(R("tint", CGI, CGI + 1), p0, 4, A.logical_shift_right)
+    ts(R("tint", CQ, CQ + 1), p0, 5, A.logical_shift_right)
+    memset(R("mul", 7, 8), 2.0 ** -11)
+    memset(R("mul", 16, 33, 16), 0.0)
+    memset(R("mul", 41, 42), 2048.0)
+    memset(R("mul", 57, 58), 0.0)
+    copy(R("col", 0, 5), R("tint", 0, 5))
+    memset(R("a0", 0, 1), 0.0)
+    ts(R("eqm"), R("krow"), col(CI), A.is_equal)
+    ts(col(C31), col(CL), -1.0, A.mult, 31.0, A.add)
+    memset(R("a1", 0, 1), 0.0)
+    scan(R("pw"), R("mul"), R("eqm"), 0.0, A.mult, A.add)
+    act(col(CB), col(CL), F.Identity, bias=-31.5)
+    act(col(CM1), col(CL), F.Identity, bias=-30720.0, scale=1024.0)
+    act(col(CW), col(CI), F.Copy, scale=524288.0)
+    act(R("a0", 385, 416), R("vrow", 0, 31), F.Abs, bias=col(C31), scale=-1.0)
+    act(R("wcon"), R("j8"), F.Identity, bias=col(CW))
+    act(R("a1", 385, 416), R("a0", 385, 416), F.Relu, bias=1024.0, scale=-1024.0)
+    act(R("ones"), R("j8", 0, 128), F.Identity, bias=1.0, scale=0.0)
+    act(R("a0", 385, 416), R("a1", 385, 416), F.Copy)
+    add("g", lambda: g.affine_select(T.ident[:], T.ones[:], [[-1, 128]], A.is_equal, 0.0, 0, 1), [R("ones")], [R("ident")])
+    act(R("r32"), R("x0", 0, 832), F.Identity, bias=1.0, scale=0.0)
+    act(R("r32", 0, 832, 32), R("j8", 0, 26), F.Copy, scale=0.0)
+    ts(R("b0", 384, 416), R("vrow", 0, 32), col(C31), A.is_equal, 1022.0, A.mult)
+    ts(col(CO), pw(PL), col(CG), A.mult)
+    ts(R("vb"), R("vrow"), pw(PSH), A.mult)
+    ts(R("b1", 384, 416), R("vrow", 0, 32), col(C31), A.is_equal, 1022.0, A.mult)
+    ts(col(CE), col(CO), -1.0, A.mult, pw(PL), A.add)
+    ts(R("vc"), R("vb"), 256, A.bitwise_and)
+    ts(R("fm", 512, 1024, 4), R("qrow"), col(CQ), A.is_equal, col(CO), A.mult)
+    ts(R("fm", 0, 512, 4), R("qrow"), col(CQ), A.is_equal, col(CE), A.mult)
+    ts(R("sg", 0, 32), R("vc", 0, 32), -1.0 / 128, A.mult, 1.0, A.add)
+    ts(R("sg", 32, 64), R("vc", 32, 64), -1.0 / 16, A.mult, 8.0, A.add)
+    ts(R("wmask"), R("grow"), col(CGI), A.is_equal, pw(PW), A.mult)
+    memset(R("bits", 1024, 1536), 0.0)
+    quant("uq", "us", "ut")
+    for k in range(4):
+        tt(R("fm", 1024 + 128 * k, 1152 + 128 * k, 4), R("sg", 0, 32), R("fm", 512 + 128 * k, 640 + 128 * k, 4), A.mult)
+        tt(R("fm", 1536 + 128 * k, 1664 + 128 * k, 4), R("sg", 32, 64), R("wmask", 32 * k, 32 * k + 32), A.mult)
+
+    quant("xq0", "xs0", "x0", *SPANS[0])
+    for t in range(ROUNDS):
+        x, xq, xs = "x%d" % t, "xq%d" % t, "xs%d" % t
+        p, pq, pp, nq, npl = "p%d" % t, "pq%d" % t, "pp%d" % t, "nq%d" % t, "np%d" % t
+        first = t == 0
+        mm(4, "uq", "us", 0, xq, xs, *SPANS[0])
+        if first:
+            quant("fq", "fs", "fm")
+        quant(xq, xs, x, *SPANS[1])
+        mm(5, "uq", "us", 0, xq, xs, *SPANS[1])
+        for b in range(2):
+            mm(b, "wq", "wp", b, xq, xs)
+        for k, (lo, hi) in enumerate(SPANS):
+            ts(R("bits", 4 * lo, 4 * hi, 4), bank(4 + k, hi - lo), 0.0, A.is_lt, pw(PS), A.mult)
+        for k, (lo, hi) in enumerate(SPANS):
+            quant("bq", "bs", "bits", lo, hi)
+            mm(2 + k, "fq", "fs", 0, "bq", "bs", lo, hi)
+        for b in range(2):
+            act(R(p, b, 4 * C, 4), bank(b), F.Copy, scale=0.03125)
+        mm(4, "fq", "fs", 0, "bq", "bs")
+        mm(7, "fq", "fs", 3, "bq", "bs")
+        mm(6, "fq", "fs", 2, "bq", "bs")
+        mm(5, "fq", "fs", 1, "bq", "bs")
+        if first:
+            ts(R("tint", 5, 6), p0, 15, A.bitwise_and, 1, A.logical_shift_right)
+            ts(R("tint", 6, 8), R("pint", 2, 4), 16, A.bitwise_and)
+        act(R("junk"), bank(4), F.Sign, bias=col(CB), acc=R("base", 0, 1))
+        act(R("a1", 1, 385), bank(6), F.Relu, bias=col(CM1), scale=-1024.0)
+        act(R("junk"), bank(5), F.Sign, bias=col(CB), acc=R("base", 1, 2))
+        for k, (lo, hi) in enumerate(SPANS):
+            ts(R("a0", 1 + lo, 1 + hi), bank(2 + k, hi - lo), col(C31), A.is_equal, 1024.0, A.mult)
+        for b in range(2, 4):
+            mm(b, "wq", "wp", b, xq, xs)
+            act(R(p, b, 4 * C, 4), bank(b), F.Copy, scale=0.03125)
+        if first:
+            copy(col(CH), R("tint", 5, 6))
+        else:
+            mm(4, "eq", "es", 4, "bq", "bs")
+        ts(R("b0", 0, 384), R("a0", 1, 385), 1022.0 / 1024, A.mult)
+        tt(R("key"), bank(7), R("wcon"), A.add)
+        scan(R("cum", 0, 416), R("a0"), R("b0"), R("base", 0, 1), A.add, A.subtract)
+        ts(R("b1", 0, 384), R("a1", 1, 385), 1022.0 / 1024, A.mult)
+        if first:
+            ts(col(CA), col(CG), 13.0, A.mult, col(CH), A.add)
+            ts(R("tint", 8, 9), p0, 3, A.logical_shift_right, 2, A.bitwise_and)
+            ts(col(CA8), col(CA), 8.0, A.add)
+        scan(R("cum", 416, 832), R("a1"), R("b1"), R("base", 1, 2), A.add, A.subtract)
+        if first:
+            ts(R("lp", 0, 1), R("tint", 6, 7), 4.0, A.mult, col(CA), A.add)
+        turn(R("zt"), R("cum"))
+        if first:
+            ts(R("lp", 1, 2), R("tint", 7, 8), 4.0, A.mult, col(CA8), A.add)
+            fill(R("zw", 26, 32), 0.0)
+            fill(R("zw", 58, 64), 0.0)
+            act(col(C64), col(CG), F.Copy, scale=64.0)
+            act(col(CNL), pw(PL), F.Copy, scale=-1.0)
+            act(col(CB2), col(CH), F.Identity, bias=col(CG), scale=2.0)
+            fill(R("ymin", 0, 3 * 392, 392), HUGE)
+            for k in range(3):
+                fill(R("ymin", 392 * k + 385, 392 * k + 392), HUGE)
+            act(col(CF), pw(PH), F.Identity, bias=col(CNL), scale=288.0)
+            act(col(CB3), col(CB2), F.Identity, bias=16.0)
+            fill(R("firsts", 64, 96), 0.0)
+            fill(R("firsts", 128, 160), 0.0)
+            fill(R("ta", 0, 64), 0.0)
+            fill(R("ta", 224, 288), 0.0)
+            act(R("em", 0, 2048), R("fm"), F.Copy, scale=0.0)
+            act(R("em", 2048, 2560), R("fm", 0, 512), F.Copy, scale=0.0)
+            for b in range(4):
+                act(R("em", 512 * b + b, 512 * b + 512, 4), R("ident"), F.Copy)
+            act(R("r16"), R("r32", 0, C), F.Copy)
+            fill(R("k512"), 512.0)
+            fill(R("r16", 16, C, 32), 0.0)
+            fill(R("dist", 34, 288, 36), 4096.0)
+            fill(R("dist", 35, 288, 36), 4096.0)
+            fill(R("dwin", 0, 4 * 392, 392), 0.0)
+            for b in range(4):
+                fill(R("dwin", 392 * b + 385, 392 * b + 392), 0.0)
+        act(R("hsg"), R("key"), F.Sign, bias=524287.5, scale=-1.0)
+        act(R("him"), R("hsg"), F.Relu)
+        scan(R("zs"), R("r32"), R("zt"), 0.0, A.mult, A.min)
+        quant(pq, pp, p)
+        send(nq, pq, "gotp%d" % t, codes=True)
+        send(npl, pp, "gotp%d" % t)
+        copy(R("zw", 0, 26), R("zs", 31, 832, 32))
+        copy(R("zw", 32, 58), R("zs", 31, 832, 32))
+        if first:
+            tt(R("tint", 9, 10), R("tint", 8, 9), R("pint", 4, 5), A.add)
+        turn(R("zu"), R("zw", 0, 64))
+        if first:
+            ts(R("tint", 10, 11), R("tint", 9, 10), 15, A.bitwise_and)
+        turn(R("zw", 64, 96), R("zu", 16, 48))
+        if first:
+            copy(col(CSH), R("tint", 10, 11))
+        ts(R("lpos"), (R("zw"), R("lp")), 1406.0, A.add, 0.5, A.mult)
+        if first:
+            ts(R("lsh"), R("row16"), col(CSH), A.add, col(C64), A.add)
+        ends = R("lpos", 24, 26)
+        copy((R("srt"), R("lpos", 0, 24)), R("key"))
+        scan(R("ymin", 1, 385), R("srt"), R("srt"), HUGE, A.min, A.min)
+        scan(R("ymin", 393, 777), R("srt"), R("ymin", 0, 384), HUGE, A.min, A.max)
+        tt(R("firsts", 32, 64), (R("ymin", 0, 392), ends), R("crow", 0, 32), A.subtract)
+        scan(R("ymin", 785, 1169), R("srt"), R("ymin", 392, 776), HUGE, A.min, A.max)
+        tt(R("firsts", 96, 128), (R("ymin", 392, 784), ends), R("crow", 32, 64), A.subtract)
+        tt(R("firsts", 160, 192), (R("ymin", 784, 1176), ends), R("crow", 32, 64), A.subtract)
+        turn(R("ta", 64, 224), R("firsts", 32, 192))
+        copy(R("tb"), (R("ta"), R("lsh")))
+        for k in (1, 2, 3, 0):
+            turn(R("firsts", 64 * k, 64 * k + 32), R("tb", 32 * k, 32 * k + 32))
+        tt(R("r1"), R("firsts", 96, 130), R("firsts", 31, 65), A.max)
+        ts(R("r2"), R("firsts", 95, 129), -4096.0, A.add)
+        tt(R("r3"), R("r1"), R("firsts", 160, 194), A.min)
+        tt(R("r4"), R("r2"), R("firsts", 30, 64), A.min)
+        tt(R("vi"), R("r3"), R("r4"), A.min)
+        ts(R("vf"), R("vi"), 0xFFC007, A.bitwise_and)
+        ts(R("vn"), R("vi"), 3, A.logical_shift_right, 511, A.bitwise_and)
+        ts(R("vg"), R("vf"), 2048.0, A.mult, 18432.0, A.min)
+        tt(R("tab%d" % t), R("vg"), R("vn"), A.add)
+        send("land%d" % t, "tab%d" % t, "gott%d" % t)
+        if first:
+            ts(R("em", 2048, 2560, 4), R("grow"), col(CGI), A.is_equal, col(CF), A.mult)
+            ts(R("diag"), R("k16"), col(CI), A.is_equal)
+            quant("eq", "es", "em", 512, 640)
+            mm(4, "eq", "es", 4, "bq", "bs")
+            quant("eq", "es", "em", 0, 512)
+        tt(R("dg"), bank(4), R("diag"), A.mult)
+        if first:
+            ts(R("lq", 0, 1), R("tint", 6, 7), 4.0, A.mult, col(CB2), A.add)
+        scan(R("dgs"), R("r16"), R("dg"), 0.0, A.mult, A.add)
+        if first:
+            ts(R("lq", 1, 2), R("tint", 7, 8), 4.0, A.mult, col(CB3), A.add)
+            memset(R("fj", 24, 32), 0)
+            memset(R("fj", 56, 64), 0)
+        else:
+            quant("vq", "vs", "vt")
+        ts(R("lask"), R("dgs", 15, C, 16), 33.0, A.add)
+        for b in range(4):
+            mm(b, "eq", "es", b, nq, npl)
+        for h in range(1, 8):
+            act(R("dist", 36 * h, 36 * h + 34), R("land%d" % t), F.Abs, bias=1.0 - 2048 * h)
+        ts(R("dist", 0, 34), R("land%d" % t), 1.0, A.add)
+        for b in range(4):
+            act(R("dwin", 392 * b + 1, 392 * b + 385), bank(b), F.Copy)
+        scan(R("ans"), R("k512"), R("dist"), 4096.0, A.add, A.min)
+        tt(R("z2"), (R("ans"), R("lask")), R("him"), A.mult)
+        turn(R("zt2"), R("z2"))
+        scan(R("zs2"), R("r16"), R("zt2"), 0.0, A.mult, A.max)
+        ts(R("fi"), R("zs2", 15, C, 16), 1536.0, A.min)
+        ts(R("fj", 0, 24), R("fi"), 511, A.bitwise_and)
+        ts(R("fj", 32, 56), R("fi"), 511, A.bitwise_and)
+        turn(R("fu"), R("fj", 0, 64))
+        turn(R("fj", 64, 96), R("fu", 16, 48))
+        copy(R("lfound"), (R("fj"), R("lq")))
+        nx = "x%d" % (t + 1)
+        for k, (lo, hi) in enumerate(SPANS):
+            for b in range(4):
+                tt(R(nx, 4 * lo + b, 4 * hi, 4), (R("dwin", 392 * b, 392 * b + 392), R("lfound", lo // 16, hi // 16)),
+                   R(p, 4 * lo + b, 4 * hi, 4), A.add)
+                if k == 1 and b == 0:
+                    quant("xq%d" % (t + 1), "xs%d" % (t + 1), nx, *SPANS[0])
+
+    x, xq, xs = "x%d" % ROUNDS, "xq%d" % ROUNDS, "xs%d" % ROUNDS
+    outs = [("out", k, k + 1, 1) for k in range(8)]
+    for k, (lo, hi) in enumerate(SPANS):
+        if k:
+            quant(xq, xs, x, lo, hi)
+        mm(5 + k, "vq", "vs", 0, xq, xs, lo, hi)
+        dma("s", lambda lo=lo, hi=hi: T.oc[:, 4 * lo:4 * hi], lambda lo=lo, hi=hi: T[xq][:, lo:hi].bitcast(dt.uint8), [R(xq, lo, hi)], [outs[k]])
+        if k:
+            for m in range(4):
+                dma("sa"[m % 2], lambda m=m: T.osc[4 * m:4 * m + 4, :], lambda m=m: T[xs][32 * m:32 * m + 4, :], [R(xs)], [outs[4 + m]])
+        act(R("yb", lo, hi), bank(5 + k, hi - lo), F.Copy)
+        dma("a", lambda lo=lo, hi=hi: T.y[:, lo:hi], lambda lo=lo, hi=hi: T.yb[:, lo:hi], [R("yb", lo, hi)], [outs[2 + k]])
+    add("g", lambda: g.wait_ge(T.sem.sent, 3 * ROUNDS * lanes_out), outs, [], "end")
+    emit(g, T, ops)

@@ -21,10 +21,10 @@ SCRATCH = {
     "pint": sb(8, "int32"), "tint": sb(12, "int32"), "col": sb(24, "float32"),
     "krow": sb(64, "float32"), "eqm": sb(64, "float32"), "mul": sb(64, "float32"), "pw": sb(64, "float32"),
     "vrow": sb(64, "float32"), "vb": sb(64, "int32"), "vc": sb(64, "int32"), "sg": sb(64, "bfloat16"),
-    "qrow": sb(128, "bfloat16"), "grow": sb(128, "bfloat16"), "wmask": sb(128, "bfloat16"),
+    "qrow": sb(128, "bfloat16"), "grow": sb(128, "bfloat16"), "wmask": sb(32, "bfloat16"), "w32": sb(32, "bfloat16"),
     "ones": sb(128, "bfloat16"), "ident": sb(128, "bfloat16"),
     "j8": sb(C, "float32"), "wcon": sb(C, "float32"), "k16": sb(C, "bfloat16"), "diag": sb(C, "bfloat16"),
-    "r32": sb(832, "bfloat16"), "r16": sb(C, "bfloat16"), "k512": sb(288, "bfloat16"),
+    "r32": sb(416, "bfloat16"), "r16": sb(C, "bfloat16"), "k512": sb(288, "bfloat16"),
     "crow": sb(64, "float32"), "row16": sb(8, "float32"), "lp": sb(2, "uint16"), "lq": sb(2, "uint16"), "lsh": sb(8, "uint16"),
     "bits": sb(4 * C, "bfloat16"), "bq": sb(C, X4), "bs": sb(C, "uint8"),
     "a0": sb(416, "bfloat16"), "a1": sb(416, "bfloat16"), "b0": sb(416, H16), "b1": sb(416, H16),
@@ -37,7 +37,7 @@ SCRATCH = {
     "hsg": sb(C, "bfloat16"), "him": sb(C, "bfloat16"), "dg": sb(C, H16), "dgs": sb(C, H16), "lask": sb(24, "uint16"),
     "dist": sb(288, "float32"), "ans": sb(288, "float32"),
     "z2": sb(C, H16), "zt2": sb(C, H16), "zs2": sb(C, H16), "fi": sb(24, "int32"), "fj": sb(96, "int32"), "fu": sb(64, "int32"),
-    "lfound": sb(32, "uint16"), "dwin": sb(4 * 392, "float32"), "yb": sb(C, "float32"),
+    "lfound": sb(32, "uint16"), "dwin": sb(4 * 392, "float32"), "mg": sb(3 * C, "bfloat16"), "yb": sb(C, "float32"),
 }
 for _t in range(ROUNDS + 1):
     SCRATCH["x%d" % _t] = sb(4 * C, "bfloat16")
@@ -88,27 +88,35 @@ def emit(g, T, ops):
         waits.append(deps)
         needed.update(deps)
         before.append(set() if kind == "arrive" else known[q])
+    team, seen = {}, set()
+    for i in range(len(ops)):
+        fresh = [j for j in waits[i] if j not in seen and ops[j][1] == "op"]
+        seen.update(waits[i])
+        for j in fresh:
+            team[j] = fresh
     last, mark = [], {}
     for i, (q, kind, fn, rd, wr) in enumerate(ops):
         if kind == "arrive":
             mark[i] = fn
             continue
-        for j in reversed(waits[i]):
-            queues[q].wait_ge(T.sem[mark[j][0]], mark[j][1])
+        for m in sorted(set(mark[j] for j in waits[i])):
+            queues[q].wait_ge(T.sem[m[0]], m[1])
         call = fn()
         if i in needed:
-            k = len(last)
-            if kind == "op":
-                for n in range(len(last)):
-                    if last[n][2] == "op" and last[n][0] in before[i]:
-                        k = n
-                        break
-            if k == len(last):
-                last.append((i, 0, kind))
-            step = 1 if kind == "op" else 16
-            last[k] = (i, last[k][1] + step, kind)
-            mark[i] = ("s%d" % k, last[k][1])
-            call.then_inc(T.sem["s%d" % k], step)
+            mates = team.get(i, [i])
+            if i not in mark:
+                k = len(last)
+                if kind == "op":
+                    for n in range(len(last)):
+                        if last[n][2] == "op" and all(j in before[m] for j in last[n][0] for m in mates):
+                            k = n
+                            break
+                if k == len(last):
+                    last.append(([], 0, kind))
+                last[k] = (mates, last[k][1] + (len(mates) if kind == "op" else 16), kind)
+                for m in mates:
+                    mark[m] = ("s%d" % k, last[k][1])
+            call.then_inc(T.sem[mark[i][0]], 1 if kind == "op" else 16)
 
 
 def rank_program(g, core, T, topo):
@@ -248,7 +256,7 @@ def rank_program(g, core, T, topo):
     iota(R("k16"), [[0, 24], [1, 16]], 0, 0)
     memset(R("fm", 0, 1024), 0.0)
     act(R("fm", 1024, 2048), R("fm", 0, 1024), F.Copy)
-    act(R("bits", 0, 1024), R("fm", 1024, 2048), F.Copy)
+    act(R("bits", 0, 768), R("fm", 1024, 1792), F.Copy)
     memset(R("mul", 0, 32), 2.0)
     memset(R("mul", 32, 64), 1.0)
     p0 = R("pint", 0, 1)
@@ -267,6 +275,24 @@ def rank_program(g, core, T, topo):
     ts(col(C31), col(CL), -1.0, A.mult, 31.0, A.add)
     memset(R("a1", 0, 1), 0.0)
     scan(R("pw"), R("mul"), R("eqm"), 0.0, A.mult, A.add)
+    ts(R("b0", 384, 416), R("vrow", 0, 32), col(C31), A.is_equal, 1022.0, A.mult)
+    ts(col(CO), pw(PL), col(CG), A.mult)
+    ts(R("vb"), R("vrow"), pw(PSH), A.mult)
+    ts(R("b1", 384, 416), R("vrow", 0, 32), col(C31), A.is_equal, 1022.0, A.mult)
+    ts(col(CE), col(CO), -1.0, A.mult, pw(PL), A.add)
+    ts(R("vc"), R("vb"), 256, A.bitwise_and)
+    ts(R("fm", 512, 1024, 4), R("qrow"), col(CQ), A.is_equal, col(CO), A.mult)
+    ts(R("sg", 32, 64), R("vc", 32, 64), -1.0 / 16, A.mult, 8.0, A.add)
+    ts(R("sg", 0, 32), R("vc", 0, 32), -1.0 / 128, A.mult, 1.0, A.add)
+    ts(R("wmask"), R("grow", 0, 32), col(CG), A.is_equal, pw(PW), A.mult)
+    ts(R("fm", 0, 512, 4), R("qrow"), col(CQ), A.is_equal, col(CE), A.mult)
+    tt(R("w32"), R("sg", 32, 64), R("wmask"), A.mult)
+    for lo in range(0, 128, 32):
+        hi = lo + 32
+        add("a", lambda lo=lo, hi=hi: S.activation(T.fm[lo:hi, 1024 + 4 * lo:1024 + 4 * hi:4], T.sg[lo:hi, 0:32], F.Identity, scale=T.col[lo:hi, CO:CO + 1]),
+            [R("sg", 0, 32), col(CO)], [R("fm", 1024 + 4 * lo, 1024 + 4 * hi, 4)])
+        add("a", lambda lo=lo, hi=hi: S.activation(T.fm[lo:hi, 1536 + 4 * lo:1536 + 4 * hi:4], T.w32[lo:hi, :], F.Copy),
+            [R("w32")], [R("fm", 1536 + 4 * lo, 1536 + 4 * hi, 4)])
     act(col(CB), col(CL), F.Identity, bias=-31.5)
     act(col(CM1), col(CL), F.Identity, bias=-30720.0, scale=1024.0)
     act(col(CW), col(CI), F.Copy, scale=524288.0)
@@ -276,88 +302,81 @@ def rank_program(g, core, T, topo):
     act(R("ones"), R("j8", 0, 128), F.Identity, bias=1.0, scale=0.0)
     act(R("a0", 385, 416), R("a1", 385, 416), F.Copy)
     add("g", lambda: g.affine_select(T.ident[:], T.ones[:], [[-1, 128]], A.is_equal, 0.0, 0, 1), [R("ones")], [R("ident")])
-    act(R("r32"), R("x0", 0, 832), F.Identity, bias=1.0, scale=0.0)
-    act(R("r32", 0, 832, 32), R("j8", 0, 26), F.Copy, scale=0.0)
-    ts(R("b0", 384, 416), R("vrow", 0, 32), col(C31), A.is_equal, 1022.0, A.mult)
-    ts(col(CO), pw(PL), col(CG), A.mult)
-    ts(R("vb"), R("vrow"), pw(PSH), A.mult)
-    ts(R("b1", 384, 416), R("vrow", 0, 32), col(C31), A.is_equal, 1022.0, A.mult)
-    ts(col(CE), col(CO), -1.0, A.mult, pw(PL), A.add)
-    ts(R("vc"), R("vb"), 256, A.bitwise_and)
-    ts(R("fm", 512, 1024, 4), R("qrow"), col(CQ), A.is_equal, col(CO), A.mult)
-    ts(R("fm", 0, 512, 4), R("qrow"), col(CQ), A.is_equal, col(CE), A.mult)
-    ts(R("sg", 0, 32), R("vc", 0, 32), -1.0 / 128, A.mult, 1.0, A.add)
-    ts(R("sg", 32, 64), R("vc", 32, 64), -1.0 / 16, A.mult, 8.0, A.add)
-    ts(R("wmask"), R("grow"), col(CGI), A.is_equal, pw(PW), A.mult)
-    memset(R("bits", 1024, 1536), 0.0)
+    act(R("zw", 26, 32), R("j8", 0, 6), F.Copy, scale=0.0)
+    act(R("r32"), R("x0", 0, 416), F.Identity, bias=1.0, scale=0.0)
+    act(R("zw", 58, 64), R("j8", 0, 6), F.Copy, scale=0.0)
+    act(R("r32", 0, 416, 32), R("j8", 0, 13), F.Copy, scale=0.0)
+    memset(R("bits", 768, 1536), 0.0)
+    quant("fq", "fs", "fm", 0, 256)
     quant("uq", "us", "ut")
-    for k in range(4):
-        tt(R("fm", 1024 + 128 * k, 1152 + 128 * k, 4), R("sg", 0, 32), R("fm", 512 + 128 * k, 640 + 128 * k, 4), A.mult)
-        tt(R("fm", 1536 + 128 * k, 1664 + 128 * k, 4), R("sg", 32, 64), R("wmask", 32 * k, 32 * k + 32), A.mult)
 
     quant("xq0", "xs0", "x0", *SPANS[0])
     for t in range(ROUNDS):
         x, xq, xs = "x%d" % t, "xq%d" % t, "xs%d" % t
         p, pq, pp, nq, npl = "p%d" % t, "pq%d" % t, "pp%d" % t, "nq%d" % t, "np%d" % t
         first = t == 0
+        early = 0 if first else 2
+
+        def send_p():
+            quant(pq, pp, p)
+            send(nq, pq, "gotp%d" % t, codes=True)
+            send(npl, pp, "gotp%d" % t)
+
         mm(4, "uq", "us", 0, xq, xs, *SPANS[0])
-        if first:
-            quant("fq", "fs", "fm")
         quant(xq, xs, x, *SPANS[1])
         mm(5, "uq", "us", 0, xq, xs, *SPANS[1])
-        for b in range(2):
+        for b in range(early):
             mm(b, "wq", "wp", b, xq, xs)
         for k, (lo, hi) in enumerate(SPANS):
             ts(R("bits", 4 * lo, 4 * hi, 4), bank(4 + k, hi - lo), 0.0, A.is_lt, pw(PS), A.mult)
         for k, (lo, hi) in enumerate(SPANS):
             quant("bq", "bs", "bits", lo, hi)
             mm(2 + k, "fq", "fs", 0, "bq", "bs", lo, hi)
-        for b in range(2):
+        if first:
+            quant("fq", "fs", "fm", 256, 512)
+        for b in range(early):
             act(R(p, b, 4 * C, 4), bank(b), F.Copy, scale=0.03125)
         mm(4, "fq", "fs", 0, "bq", "bs")
         mm(7, "fq", "fs", 3, "bq", "bs")
         mm(6, "fq", "fs", 2, "bq", "bs")
         mm(5, "fq", "fs", 1, "bq", "bs")
-        if first:
-            ts(R("tint", 5, 6), p0, 15, A.bitwise_and, 1, A.logical_shift_right)
-            ts(R("tint", 6, 8), R("pint", 2, 4), 16, A.bitwise_and)
         act(R("junk"), bank(4), F.Sign, bias=col(CB), acc=R("base", 0, 1))
         act(R("a1", 1, 385), bank(6), F.Relu, bias=col(CM1), scale=-1024.0)
         act(R("junk"), bank(5), F.Sign, bias=col(CB), acc=R("base", 1, 2))
         for k, (lo, hi) in enumerate(SPANS):
             ts(R("a0", 1 + lo, 1 + hi), bank(2 + k, hi - lo), col(C31), A.is_equal, 1024.0, A.mult)
-        for b in range(2, 4):
+        for b in range(early, 4):
             mm(b, "wq", "wp", b, xq, xs)
             act(R(p, b, 4 * C, 4), bank(b), F.Copy, scale=0.03125)
         if first:
-            copy(col(CH), R("tint", 5, 6))
+            ts(R("tint", 5, 6), p0, 15, A.bitwise_and, 1, A.logical_shift_right)
         else:
             mm(4, "eq", "es", 4, "bq", "bs")
         ts(R("b0", 0, 384), R("a0", 1, 385), 1022.0 / 1024, A.mult)
         tt(R("key"), bank(7), R("wcon"), A.add)
         scan(R("cum", 0, 416), R("a0"), R("b0"), R("base", 0, 1), A.add, A.subtract)
+        if first:
+            copy(col(CH), R("tint", 5, 6))
         ts(R("b1", 0, 384), R("a1", 1, 385), 1022.0 / 1024, A.mult)
         if first:
             ts(col(CA), col(CG), 13.0, A.mult, col(CH), A.add)
-            ts(R("tint", 8, 9), p0, 3, A.logical_shift_right, 2, A.bitwise_and)
-            ts(col(CA8), col(CA), 8.0, A.add)
+            ts(R("tint", 6, 8), R("pint", 2, 4), 16, A.bitwise_and)
+        turn(R("zt", 0, 416), R("cum", 0, 416))
         scan(R("cum", 416, 832), R("a1"), R("b1"), R("base", 1, 2), A.add, A.subtract)
+        scan(R("zs", 0, 416), R("r32"), R("zt", 0, 416), 0.0, A.mult, A.min)
+        turn(R("zt", 416, 832), R("cum", 416, 832))
         if first:
+            ts(col(CA8), col(CA), 8.0, A.add)
             ts(R("lp", 0, 1), R("tint", 6, 7), 4.0, A.mult, col(CA), A.add)
-        turn(R("zt"), R("cum"))
-        if first:
-            ts(R("lp", 1, 2), R("tint", 7, 8), 4.0, A.mult, col(CA8), A.add)
-            fill(R("zw", 26, 32), 0.0)
-            fill(R("zw", 58, 64), 0.0)
-            act(col(C64), col(CG), F.Copy, scale=64.0)
-            act(col(CNL), pw(PL), F.Copy, scale=-1.0)
-            act(col(CB2), col(CH), F.Identity, bias=col(CG), scale=2.0)
             fill(R("ymin", 0, 3 * 392, 392), HUGE)
             for k in range(3):
                 fill(R("ymin", 392 * k + 385, 392 * k + 392), HUGE)
+            act(col(C64), col(CG), F.Copy, scale=64.0)
+            act(col(CNL), pw(PL), F.Copy, scale=-1.0)
+            act(col(CB2), col(CH), F.Identity, bias=col(CG), scale=2.0)
+            fill(R("firsts", 64, 96), 0.0)
             act(col(CF), pw(PH), F.Identity, bias=col(CNL), scale=288.0)
             act(col(CB3), col(CB2), F.Identity, bias=16.0)
-            fill(R("firsts", 64, 96), 0.0)
             fill(R("firsts", 128, 160), 0.0)
             fill(R("ta", 0, 64), 0.0)
             fill(R("ta", 224, 288), 0.0)
@@ -375,26 +394,31 @@ def rank_program(g, core, T, topo):
                 fill(R("dwin", 392 * b + 385, 392 * b + 392), 0.0)
         act(R("hsg"), R("key"), F.Sign, bias=524287.5, scale=-1.0)
         act(R("him"), R("hsg"), F.Relu)
-        scan(R("zs"), R("r32"), R("zt"), 0.0, A.mult, A.min)
-        quant(pq, pp, p)
-        send(nq, pq, "gotp%d" % t, codes=True)
-        send(npl, pp, "gotp%d" % t)
+        scan(R("zs", 416, 832), R("r32"), R("zt", 416, 832), 0.0, A.mult, A.min)
+        if first:
+            ts(R("lp", 1, 2), R("tint", 7, 8), 4.0, A.mult, col(CA8), A.add)
+        else:
+            send_p()
         copy(R("zw", 0, 26), R("zs", 31, 832, 32))
         copy(R("zw", 32, 58), R("zs", 31, 832, 32))
         if first:
-            tt(R("tint", 9, 10), R("tint", 8, 9), R("pint", 4, 5), A.add)
+            ts(R("tint", 8, 9), p0, 3, A.logical_shift_right, 2, A.bitwise_and)
         turn(R("zu"), R("zw", 0, 64))
         if first:
-            ts(R("tint", 10, 11), R("tint", 9, 10), 15, A.bitwise_and)
+            tt(R("tint", 9, 10), R("tint", 8, 9), R("pint", 4, 5), A.add)
         turn(R("zw", 64, 96), R("zu", 16, 48))
         if first:
-            copy(col(CSH), R("tint", 10, 11))
+            ts(R("tint", 10, 11), R("tint", 9, 10), 15, A.bitwise_and)
         ts(R("lpos"), (R("zw"), R("lp")), 1406.0, A.add, 0.5, A.mult)
         if first:
-            ts(R("lsh"), R("row16"), col(CSH), A.add, col(C64), A.add)
+            send_p()
         ends = R("lpos", 24, 26)
         copy((R("srt"), R("lpos", 0, 24)), R("key"))
+        if first:
+            copy(col(CSH), R("tint", 10, 11))
         scan(R("ymin", 1, 385), R("srt"), R("srt"), HUGE, A.min, A.min)
+        if first:
+            ts(R("lsh"), R("row16"), col(CSH), A.add, col(C64), A.add)
         scan(R("ymin", 393, 777), R("srt"), R("ymin", 0, 384), HUGE, A.min, A.max)
         tt(R("firsts", 32, 64), (R("ymin", 0, 392), ends), R("crow", 0, 32), A.subtract)
         scan(R("ymin", 785, 1169), R("srt"), R("ymin", 392, 776), HUGE, A.min, A.max)
@@ -439,9 +463,12 @@ def rank_program(g, core, T, topo):
         for b in range(4):
             act(R("dwin", 392 * b + 1, 392 * b + 385), bank(b), F.Copy)
         scan(R("ans"), R("k512"), R("dist"), 4096.0, A.add, A.min)
-        tt(R("z2"), (R("ans"), R("lask")), R("him"), A.mult)
-        turn(R("zt2"), R("z2"))
-        scan(R("zs2"), R("r16"), R("zt2"), 0.0, A.mult, A.max)
+        for lo, hi in SPANS:
+            tt(R("z2", lo, hi), (R("ans"), R("lask", lo // 16, hi // 16)), R("him", lo, hi), A.mult)
+        for lo, hi in SPANS:
+            turn(R("zt2", lo, hi), R("z2", lo, hi))
+        for lo, hi in SPANS:
+            scan(R("zs2", lo, hi), R("r16", lo, hi), R("zt2", lo, hi), 0.0, A.mult, A.max)
         ts(R("fi"), R("zs2", 15, C, 16), 1536.0, A.min)
         ts(R("fj", 0, 24), R("fi"), 511, A.bitwise_and)
         ts(R("fj", 32, 56), R("fi"), 511, A.bitwise_and)
@@ -450,9 +477,12 @@ def rank_program(g, core, T, topo):
         copy(R("lfound"), (R("fj"), R("lq")))
         nx = "x%d" % (t + 1)
         for k, (lo, hi) in enumerate(SPANS):
+            found = R("lfound", lo // 16, hi // 16)
+            for b in range(2 - k, 4):
+                act(R("mg", C * (b - 1) + lo, C * (b - 1) + hi), (R("dwin", 392 * b, 392 * b + 392), found), F.Copy)
             for b in range(4):
-                tt(R(nx, 4 * lo + b, 4 * hi, 4), (R("dwin", 392 * b, 392 * b + 392), R("lfound", lo // 16, hi // 16)),
-                   R(p, 4 * lo + b, 4 * hi, 4), A.add)
+                src = (R("dwin", 392 * b, 392 * b + 392), found) if b < 2 - k else R("mg", C * (b - 1) + lo, C * (b - 1) + hi)
+                tt(R(nx, 4 * lo + b, 4 * hi, 4), src, R(p, 4 * lo + b, 4 * hi, 4), A.add)
                 if k == 1 and b == 0:
                     quant("xq%d" % (t + 1), "xs%d" % (t + 1), nx, *SPANS[0])
 

@@ -3,9 +3,13 @@ from concourse.mybir import dt, AluOpType as A, ActivationFunctionType as F
 C = 384
 ROUNDS = 2
 H16 = "float16"
-HUGE = 8388608.0
 X4 = "float8_e4m3fn_x4"
 SPANS = ((0, 256), (256, C))
+UP = 2048.0
+MISS = 524288.0
+MID = 8192.0 * 31 + 2 * MISS + 3.5
+HUGE = UP * (MISS - MID)
+TINY = 1e-37
 
 
 def sb(n, dtype):
@@ -16,28 +20,27 @@ SCRATCH = {
     "ps": ("psum", [128, 4096], "float32"),
     "ut": sb(512, "bfloat16"), "vt": sb(512, "bfloat16"), "uq": sb(128, X4), "us": sb(128, "uint8"),
     "vq": sb(128, X4), "vs": sb(128, "uint8"), "wq": sb(512, X4), "wp": sb(512, "uint8"),
-    "fm": sb(2048, "bfloat16"), "fq": sb(512, X4), "fs": sb(512, "uint8"),
+    "fm": sb(2560, "bfloat16"), "fq": sb(640, X4), "fs": sb(640, "uint8"),
     "em": sb(2560, "bfloat16"), "eq": sb(640, X4), "es": sb(640, "uint8"),
     "pint": sb(8, "int32"), "tint": sb(12, "int32"), "col": sb(24, "float32"),
-    "krow": sb(64, "float32"), "eqm": sb(64, "float32"), "mul": sb(64, "float32"), "pw": sb(64, "float32"),
+    "krow": sb(48, "float32"), "eqm": sb(48, "float32"), "mul": sb(48, "float32"), "pw": sb(48, "float32"),
     "vrow": sb(64, "float32"), "vb": sb(64, "int32"), "vc": sb(64, "int32"), "sg": sb(64, "bfloat16"),
     "qrow": sb(128, "bfloat16"), "grow": sb(128, "bfloat16"), "wmask": sb(32, "bfloat16"), "w32": sb(32, "bfloat16"),
     "ones": sb(128, "bfloat16"), "ident": sb(128, "bfloat16"),
-    "j8": sb(C, "float32"), "wcon": sb(C, "float32"), "k16": sb(C, "bfloat16"), "diag": sb(C, "bfloat16"),
-    "r32": sb(416, "bfloat16"), "r16": sb(C, "bfloat16"), "k512": sb(288, "bfloat16"),
-    "crow": sb(64, "float32"), "row16": sb(8, "float32"), "lp": sb(2, "uint16"), "lq": sb(2, "uint16"), "lsh": sb(8, "uint16"),
+    "wcon": sb(C, "float32"), "k16": sb(C, "bfloat16"), "diag": sb(C, "bfloat16"),
+    "r32": sb(416, "bfloat16"), "r16": sb(C, "bfloat16"), "k512": sb(144, "bfloat16"),
+    "crow": sb(64, "float32"), "row16": sb(8, "float32"), "lq": sb(2, "uint16"), "lsh": sb(8, "uint16"),
     "bits": sb(4 * C, "bfloat16"), "bq": sb(C, X4), "bs": sb(C, "uint8"),
     "a0": sb(416, "bfloat16"), "a1": sb(416, "bfloat16"), "b0": sb(416, H16), "b1": sb(416, H16),
-    "cum": sb(832, H16), "base": sb(2, "float32"), "junk": sb(C, "bfloat16"),
-    "key": sb(C, "float32"), "srt": sb(C, "float32"), "zt": sb(832, H16), "zs": sb(832, H16),
-    "zw": sb(96, "float32"), "zu": sb(64, "float32"), "lpos": sb(32, "uint16"),
-    "ymin": sb(3 * 392, "float32"), "firsts": sb(224, "float32"), "ta": sb(288, "float32"), "tb": sb(128, "float32"),
+    "cnt": sb(832, H16), "cum": ("sbuf", [128, 26, 32], H16), "base": sb(2, "float32"), "junk": sb(2 * C, "bfloat16"),
+    "key": sb(C, "float32"), "srt": sb(C, "float32"), "zt": sb(832, H16), "zs": sb(832, H16), "lpos": sb(32, "uint16"),
+    "ymin": sb(3 * 392, "float32"), "firsts": sb(224, "float32"), "ta": sb(320, "float32"), "tb": sb(128, "float32"),
     "r1": sb(34, "float32"), "r2": sb(34, "float32"), "r3": sb(34, "float32"), "r4": sb(34, "float32"),
-    "vi": sb(34, "int32"), "vf": sb(34, "int32"), "vn": sb(34, "int32"), "vg": sb(34, "float32"),
-    "hsg": sb(C, "bfloat16"), "him": sb(C, "bfloat16"), "dg": sb(C, H16), "dgs": sb(C, H16), "lask": sb(24, "uint16"),
+    "vi": sb(34, "int32"), "vf": sb(34, "int32"), "vn": sb(34, "int32"),
+    "him": sb(C, "bfloat16"), "dg": sb(C, H16), "dgs": sb(C, H16), "lask": sb(24, "uint16"),
     "dist": sb(288, "float32"), "ans": sb(288, "float32"),
     "z2": sb(C, H16), "zt2": sb(C, H16), "zs2": sb(C, H16), "fi": sb(24, "int32"), "fj": sb(96, "int32"), "fu": sb(64, "int32"),
-    "lfound": sb(32, "uint16"), "dwin": sb(4 * 392, "float32"), "mg": sb(3 * C, "bfloat16"), "yb": sb(C, "float32"),
+    "lfound": sb(32, "uint16"), "dwin": sb(4 * 392, "float32"), "mg": sb(4 * C, "bfloat16"), "yb": sb(C, "float32"),
 }
 for _t in range(ROUNDS + 1):
     SCRATCH["x%d" % _t] = sb(4 * C, "bfloat16")
@@ -55,8 +58,8 @@ for _t in range(ROUNDS):
 NPOOL = 120
 SEMAPHORES = ["s%d" % _i for _i in range(NPOOL)] + ["sent"] + ["gotp%d" % _t for _t in range(ROUNDS)] + ["gott%d" % _t for _t in range(ROUNDS)]
 
-CI, CL, CG, CGI, CQ, CB2, CB3, C31, CB, CM1, CW, CNL, CF, CSH, CO, CE, C64, CH, CA, CA8 = range(20)
-PS, PSH, PL, PW, PH = 15, 24, 36, 43, 59
+CI, CL, CG, CGI, CQ, CB2, CB3, C31, CB, CEQ, CW, CNL, CF, CSH, CO, CE, C64, CH = range(18)
+WLO, WF, W9, PSH = 15, 6, 31, 40
 
 
 def meet(r, s):
@@ -149,6 +152,8 @@ def rank_program(g, core, T, topo):
             return r
         if len(r) == 2:
             return ap(r[0]).indirect(ap(r[1]))
+        if r[0] == "cum":
+            return T.cum[:, :, 16 * r[1]:16 * r[1] + 16] if r[3] == 2 else T.cum[:, r[1] // 32:r[2] // 32, :]
         return T[r[0]][:, r[1]:r[2]:r[3]] if r[3] > 1 else T[r[0]][:, r[1]:r[2]]
 
     def runs(*rs):
@@ -203,10 +208,16 @@ def rank_program(g, core, T, topo):
     def fill(o, c):
         act(o, R("r32", 0, len(range(o[1], o[2], o[3]))), F.Identity, bias=c, scale=0.0)
 
-    def mm(k, lq, ls, at, rq, rs, lo=0, hi=C):
+    def mm(k, lq, ls, at, rq, rs, lo=0, hi=C, tiles=1):
         o = bank(k, hi - lo)
-        four = [R(lq, 128 * at, 128 * at + 128), R(ls, 128 * at, 128 * at + 128), R(rq, lo, hi), R(rs, lo, hi)]
-        add("t", lambda: PE.matmul_mx(ap(o), *[ap(r) for r in four], True, True), four, [o])
+        rd = [R(lq, 128 * at, 128 * (at + tiles)), R(ls, 128 * at, 128 * (at + tiles)), R(rq, lo, hi), R(rs, lo, hi)]
+
+        def call():
+            for m in range(at, at + tiles):
+                last = PE.matmul_mx(ap(o), ap(R(lq, 128 * m, 128 * m + 128)), ap(R(ls, 128 * m, 128 * m + 128)), ap(rd[2]), ap(rd[3]),
+                                    m == at, m == at + tiles - 1)
+            return last
+        add("t", call, rd, [o])
 
     def iota(o, pattern, base, mult):
         if SCRATCH[o[0]][2] == "int32":
@@ -218,13 +229,13 @@ def rank_program(g, core, T, topo):
         eng = {"a": S, "s": g.sync}[q]
         add(q, lambda: eng.dma_start(out(), in_()), rd, wr, "dma")
 
-    def send(dst, src, sem, codes=False):
+    def send(dst, src, sem, lo=0, hi=None, codes=False):
         def call():
-            o, i = ap(R(dst)), ap(R(src))
+            o, i = ap(R(dst, lo, hi)), ap(R(src, lo, hi))
             if codes:
                 o, i = o.bitcast(dt.uint8), i.bitcast(dt.uint8)
             return g.remote_dma(o, i, T.sem[sem], T.sem.sent, pid, rid, mask)
-        add("g", call, [R(src)], [], "send")
+        add("g", call, [R(src, lo, hi)], [], "send")
 
     def arrive(sem, count, bufs):
         add("g", (sem, count), [], [R(b) for b in bufs], "arrive")
@@ -237,75 +248,68 @@ def rank_program(g, core, T, topo):
         dma("s", lambda lo=lo: T.wq[:, lo:lo + 256].bitcast(dt.uint8), lambda lo=lo: T.wc[:, 4 * lo:4 * lo + 1024], [], [R("wq", lo, lo + 256)])
     dma("s", lambda: T.vt[:], lambda: T.v[:], [], [R("vt")])
     for t in range(ROUNDS):
-        arrive("gotp%d" % t, 2 * lanes_in, ["nq%d" % t, "np%d" % t])
+        arrive("gotp%d" % t, 3 * lanes_in, ["nq%d" % t, "np%d" % t])
         arrive("gott%d" % t, lanes_in, ["land%d" % t])
 
     iota(R("pint", 0, 1), [[0, 1]], 0, 1)
-    iota(R("krow", 0, 16), [[-1, 16]], 15, 0)
-    iota(R("krow", 16, 64), [[0, 3], [1, 16]], 0, 0)
+    iota(R("krow", 0, 32), [[0, 2], [-1, 16]], 15, 0)
+    iota(R("krow", 32, 48), [[1, 16]], 0, 0)
     iota(R("vrow", 0, 32), [[-1, 32]], 31, 0)
     iota(R("vrow", 32, 64), [[0, 2], [32, 16]], 0, 0)
     iota(R("qrow"), [[1, 4], [0, 32]], 0, 0)
     iota(R("grow"), [[1, 8], [0, 16]], 0, 0)
-    iota(R("j8"), [[8, C]], 0, 0)
+    iota(R("wcon"), [[8 * int(UP), C]], 0, 0)
+    iota(R("r32"), [[0, 13], [-2048, 32]], 0, 0)
     iota(R("pint", 2, 4), [[0, 2]], 0, 17)
     iota(R("pint", 4, 5), [[0, 1]], 15, 1)
     iota(R("row16"), [[64, 4], [16, 2]], 0, 0)
-    iota(R("crow", 0, 32), [[-16384, 32]], 16384 * 31, 0)
-    iota(R("crow", 32, 64), [[-16384, 32]], 16384 * 31 - 8192, 0)
     iota(R("k16"), [[0, 24], [1, 16]], 0, 0)
     memset(R("fm", 0, 1024), 0.0)
     act(R("fm", 1024, 2048), R("fm", 0, 1024), F.Copy)
+    act(R("fm", 2048, 2560), R("fm", 1024, 1536), F.Copy)
     act(R("bits", 0, 768), R("fm", 1024, 1792), F.Copy)
-    memset(R("mul", 0, 32), 2.0)
-    memset(R("mul", 32, 64), 1.0)
+    memset(R("mul"), 2.0)
     p0 = R("pint", 0, 1)
     ts(R("tint", CI, CI + 1), p0, 15, A.bitwise_and)
     ts(R("tint", CL, CL + 1), p0, 31, A.bitwise_and)
+    memset(R("mul", 16, 27), 1.0)
     ts(R("tint", CG, CG + 1), p0, 4, A.logical_shift_right, 1, A.bitwise_and)
     ts(R("tint", CGI, CGI + 1), p0, 4, A.logical_shift_right)
     ts(R("tint", CQ, CQ + 1), p0, 5, A.logical_shift_right)
-    memset(R("mul", 7, 8), 2.0 ** -11)
-    memset(R("mul", 16, 33, 16), 0.0)
-    memset(R("mul", 41, 42), 2048.0)
-    memset(R("mul", 57, 58), 0.0)
+    memset(R("mul", 4, 12, 7), 0.0)
+    memset(R("mul", 23, 33, 9), 0.0)
     copy(R("col", 0, 5), R("tint", 0, 5))
     memset(R("a0", 0, 1), 0.0)
+    memset(R("a1", 0, 1), 0.0)
     ts(R("eqm"), R("krow"), col(CI), A.is_equal)
     ts(col(C31), col(CL), -1.0, A.mult, 31.0, A.add)
-    memset(R("a1", 0, 1), 0.0)
+    memset(R("ones"), 1.0)
     scan(R("pw"), R("mul"), R("eqm"), 0.0, A.mult, A.add)
     ts(R("b0", 384, 416), R("vrow", 0, 32), col(C31), A.is_equal, 1022.0, A.mult)
-    ts(col(CO), pw(PL), col(CG), A.mult)
-    ts(R("vb"), R("vrow"), pw(PSH), A.mult)
     ts(R("b1", 384, 416), R("vrow", 0, 32), col(C31), A.is_equal, 1022.0, A.mult)
-    ts(col(CE), col(CO), -1.0, A.mult, pw(PL), A.add)
+    ts(col(CO), pw(WLO), col(CG), A.mult)
+    ts(R("vb"), R("vrow"), pw(PSH), A.mult)
+    ts(col(CW), pw(WF), -UP / 2, A.mult)
+    ts(col(CE), col(CO), -1.0, A.mult, pw(WLO), A.add)
     ts(R("vc"), R("vb"), 256, A.bitwise_and)
     ts(R("fm", 512, 1024, 4), R("qrow"), col(CQ), A.is_equal, col(CO), A.mult)
-    ts(R("sg", 32, 64), R("vc", 32, 64), -1.0 / 16, A.mult, 8.0, A.add)
+    ts(R("wmask"), R("grow", 0, 32), col(CG), A.is_equal, pw(W9), A.mult)
+    ts(R("sg", 32, 64), R("vc", 32, 64), 64 * UP, A.mult, -8192 * UP, A.add)
     ts(R("sg", 0, 32), R("vc", 0, 32), -1.0 / 128, A.mult, 1.0, A.add)
-    ts(R("wmask"), R("grow", 0, 32), col(CG), A.is_equal, pw(PW), A.mult)
     ts(R("fm", 0, 512, 4), R("qrow"), col(CQ), A.is_equal, col(CE), A.mult)
     tt(R("w32"), R("sg", 32, 64), R("wmask"), A.mult)
+    ts(R("fm", 2048, 2560, 4), R("grow"), col(CGI), A.is_equal, col(CW), A.mult)
     for lo in range(0, 128, 32):
         hi = lo + 32
         add("a", lambda lo=lo, hi=hi: S.activation(T.fm[lo:hi, 1024 + 4 * lo:1024 + 4 * hi:4], T.sg[lo:hi, 0:32], F.Identity, scale=T.col[lo:hi, CO:CO + 1]),
             [R("sg", 0, 32), col(CO)], [R("fm", 1024 + 4 * lo, 1024 + 4 * hi, 4)])
         add("a", lambda lo=lo, hi=hi: S.activation(T.fm[lo:hi, 1536 + 4 * lo:1536 + 4 * hi:4], T.w32[lo:hi, :], F.Copy),
             [R("w32")], [R("fm", 1536 + 4 * lo, 1536 + 4 * hi, 4)])
-    act(col(CB), col(CL), F.Identity, bias=-31.5)
-    act(col(CM1), col(CL), F.Identity, bias=-30720.0, scale=1024.0)
-    act(col(CW), col(CI), F.Copy, scale=524288.0)
     act(R("a0", 385, 416), R("vrow", 0, 31), F.Abs, bias=col(C31), scale=-1.0)
-    act(R("wcon"), R("j8"), F.Identity, bias=col(CW))
+    act(col(CB), col(CL), F.Identity, bias=-32.0, scale=2.0)
+    act(col(CEQ), col(CL), F.Identity, bias=-31.0, scale=2.0)
     act(R("a1", 385, 416), R("a0", 385, 416), F.Relu, bias=1024.0, scale=-1024.0)
-    act(R("ones"), R("j8", 0, 128), F.Identity, bias=1.0, scale=0.0)
-    act(R("a0", 385, 416), R("a1", 385, 416), F.Copy)
     add("g", lambda: g.affine_select(T.ident[:], T.ones[:], [[-1, 128]], A.is_equal, 0.0, 0, 1), [R("ones")], [R("ident")])
-    act(R("zw", 26, 32), R("j8", 0, 6), F.Copy, scale=0.0)
-    act(R("r32"), R("x0", 0, 416), F.Identity, bias=1.0, scale=0.0)
-    act(R("zw", 58, 64), R("j8", 0, 6), F.Copy, scale=0.0)
-    act(R("r32", 0, 416, 32), R("j8", 0, 13), F.Copy, scale=0.0)
     memset(R("bits", 768, 1536), 0.0)
     quant("fq", "fs", "fm", 0, 256)
     quant("uq", "us", "ut")
@@ -315,156 +319,169 @@ def rank_program(g, core, T, topo):
         x, xq, xs = "x%d" % t, "xq%d" % t, "xs%d" % t
         p, pq, pp, nq, npl = "p%d" % t, "pq%d" % t, "pp%d" % t, "nq%d" % t, "np%d" % t
         first = t == 0
-        early = 0 if first else 2
+        s0, s1 = SPANS
 
-        def send_p():
-            quant(pq, pp, p)
-            send(nq, pq, "gotp%d" % t, codes=True)
-            send(npl, pp, "gotp%d" % t)
-
-        mm(4, "uq", "us", 0, xq, xs, *SPANS[0])
-        quant(xq, xs, x, *SPANS[1])
-        mm(5, "uq", "us", 0, xq, xs, *SPANS[1])
-        for b in range(early):
-            mm(b, "wq", "wp", b, xq, xs)
-        for k, (lo, hi) in enumerate(SPANS):
-            ts(R("bits", 4 * lo, 4 * hi, 4), bank(4 + k, hi - lo), 0.0, A.is_lt, pw(PS), A.mult)
-        for k, (lo, hi) in enumerate(SPANS):
-            quant("bq", "bs", "bits", lo, hi)
-            mm(2 + k, "fq", "fs", 0, "bq", "bs", lo, hi)
-        if first:
-            quant("fq", "fs", "fm", 256, 512)
-        for b in range(early):
-            act(R(p, b, 4 * C, 4), bank(b), F.Copy, scale=0.03125)
-        mm(4, "fq", "fs", 0, "bq", "bs")
-        mm(7, "fq", "fs", 3, "bq", "bs")
-        mm(6, "fq", "fs", 2, "bq", "bs")
-        mm(5, "fq", "fs", 1, "bq", "bs")
-        act(R("junk"), bank(4), F.Sign, bias=col(CB), acc=R("base", 0, 1))
-        act(R("a1", 1, 385), bank(6), F.Relu, bias=col(CM1), scale=-1024.0)
-        act(R("junk"), bank(5), F.Sign, bias=col(CB), acc=R("base", 1, 2))
-        for k, (lo, hi) in enumerate(SPANS):
-            ts(R("a0", 1 + lo, 1 + hi), bank(2 + k, hi - lo), col(C31), A.is_equal, 1024.0, A.mult)
-        for b in range(early, 4):
+        def layer(b):
             mm(b, "wq", "wp", b, xq, xs)
             act(R(p, b, 4 * C, 4), bank(b), F.Copy, scale=0.03125)
+
+        def key(lo, hi):
+            tt(R("key", lo, hi), R("ps", 512 * 7 + lo, 512 * 7 + hi), R("wcon", lo, hi), A.add)
+
+        mm(4, "uq", "us", 0, xq, xs, *s0)
+        quant(xq, xs, x, *s1)
+        mm(5, "uq", "us", 0, xq, xs, *s1)
+        for k, (lo, hi) in enumerate(SPANS):
+            act(R("bits", 4 * lo, 4 * hi, 4), bank(4 + k, hi - lo), F.Sign, bias=TINY)
         if first:
-            ts(R("tint", 5, 6), p0, 15, A.bitwise_and, 1, A.logical_shift_right)
+            act(R("a0", 385, 416), R("a1", 385, 416), F.Copy)
+            quant("fq", "fs", "fm", 256, 640)
         else:
+            layer(0)
+        quant("bq", "bs", "bits", *s0)
+        mm(2, "fq", "fs", 0, "bq", "bs", *s0)
+        mm(6, "fq", "fs", 2, "bq", "bs", *s0)
+        quant("bq", "bs", "bits", *s1)
+        mm(3, "fq", "fs", 0, "bq", "bs", *s1)
+        mm(4, "fq", "fs", 0, "bq", "bs")
+        mm(1, "fq", "fs", 2, "bq", "bs", *s1)
+        mm(5, "fq", "fs", 1, "bq", "bs")
+        mm(7, "fq", "fs", 3, "bq", "bs", tiles=2)
+        ts(R("a0", 1, 1 + s0[1]), bank(2, s0[1]), col(CEQ), A.is_equal, 1024.0, A.mult)
+        act(R("a1", 1, 1 + s0[1]), bank(6, s0[1]), F.Relu, bias=-512.0 * 29, scale=512.0)
+        act(R("junk", 0, C), bank(4), F.Sign, bias=col(CB), scale=-1.0, acc=R("base", 0, 1))
+        act(R("junk", C, 2 * C), bank(5), F.Sign, bias=col(CB), scale=-1.0, acc=R("base", 1, 2))
+        ts(R("a0", 1 + s1[0], 1 + C), bank(3, C - s1[0]), col(CEQ), A.is_equal, 1024.0, A.mult)
+        ts(R("a1", 1 + s1[0], 1 + C), bank(1, C - s1[0]), 31.0, A.is_equal, 1024.0, A.mult)
+        ts(R("b0", 0, C), R("a0", 1, 1 + C), 1022.0 / 1024, A.mult)
+        ts(R("b1", 0, C), R("a1", 1, 1 + C), 1022.0 / 1024, A.mult)
+        for b in ((0, 3, 1, 2) if first else (3, 1, 2)):
+            layer(b)
+        if not first:
             mm(4, "eq", "es", 4, "bq", "bs")
-        ts(R("b0", 0, 384), R("a0", 1, 385), 1022.0 / 1024, A.mult)
-        tt(R("key"), bank(7), R("wcon"), A.add)
-        scan(R("cum", 0, 416), R("a0"), R("b0"), R("base", 0, 1), A.add, A.subtract)
+        scan(R("cnt", 0, 416), R("a0"), R("b0"), R("base", 0, 1), A.add, A.subtract)
+        key(0, 128)
+        copy(R("cum", 0, 832, 2), R("cnt", 0, 416))
+        scan(R("cnt", 416, 832), R("a1"), R("b1"), R("base", 1, 2), A.add, A.subtract)
+        key(128, 256)
+        copy(R("cum", 1, 832, 2), R("cnt", 416, 832))
+        key(256, C)
+        act(R("him"), R("key"), F.Relu, bias=MISS - MID, scale=-1.0 / UP)
         if first:
-            copy(col(CH), R("tint", 5, 6))
-        ts(R("b1", 0, 384), R("a1", 1, 385), 1022.0 / 1024, A.mult)
-        if first:
-            ts(col(CA), col(CG), 13.0, A.mult, col(CH), A.add)
-            ts(R("tint", 6, 8), R("pint", 2, 4), 16, A.bitwise_and)
-        turn(R("zt", 0, 416), R("cum", 0, 416))
-        scan(R("cum", 416, 832), R("a1"), R("b1"), R("base", 1, 2), A.add, A.subtract)
-        scan(R("zs", 0, 416), R("r32"), R("zt", 0, 416), 0.0, A.mult, A.min)
-        turn(R("zt", 416, 832), R("cum", 416, 832))
-        if first:
-            ts(col(CA8), col(CA), 8.0, A.add)
-            ts(R("lp", 0, 1), R("tint", 6, 7), 4.0, A.mult, col(CA), A.add)
             fill(R("ymin", 0, 3 * 392, 392), HUGE)
             for k in range(3):
                 fill(R("ymin", 392 * k + 385, 392 * k + 392), HUGE)
+            act(R("crow", 0, 32), R("vrow", 0, 32), F.Identity, bias=-UP * MID, scale=16384 * UP)
+            act(R("crow", 32, 64), R("vrow", 0, 32), F.Identity, bias=-UP * (MID + 8192), scale=16384 * UP)
             act(col(C64), col(CG), F.Copy, scale=64.0)
-            act(col(CNL), pw(PL), F.Copy, scale=-1.0)
-            act(col(CB2), col(CH), F.Identity, bias=col(CG), scale=2.0)
             fill(R("firsts", 64, 96), 0.0)
-            act(col(CF), pw(PH), F.Identity, bias=col(CNL), scale=288.0)
-            act(col(CB3), col(CB2), F.Identity, bias=16.0)
-            fill(R("firsts", 128, 160), 0.0)
             fill(R("ta", 0, 64), 0.0)
-            fill(R("ta", 224, 288), 0.0)
-            act(R("em", 0, 2048), R("fm"), F.Copy, scale=0.0)
+            fill(R("ta", 160, 224), 0.0)
+            fill(R("ta", 256, 320), 0.0)
+            act(col(CNL), pw(WLO), F.Copy, scale=0.5)
             act(R("em", 2048, 2560), R("fm", 0, 512), F.Copy, scale=0.0)
+            act(col(CF), pw(WF), F.Identity, bias=col(CNL), scale=-18.0)
+            act(R("em", 0, 2048), R("fm", 0, 2048), F.Copy, scale=0.0)
+            act(R("r16"), R("k16"), F.Sign)
             for b in range(4):
                 act(R("em", 512 * b + b, 512 * b + 512, 4), R("ident"), F.Copy)
-            act(R("r16"), R("r32", 0, C), F.Copy)
             fill(R("k512"), 512.0)
-            fill(R("r16", 16, C, 32), 0.0)
             fill(R("dist", 34, 288, 36), 4096.0)
             fill(R("dist", 35, 288, 36), 4096.0)
             fill(R("dwin", 0, 4 * 392, 392), 0.0)
             for b in range(4):
                 fill(R("dwin", 392 * b + 385, 392 * b + 392), 0.0)
-        act(R("hsg"), R("key"), F.Sign, bias=524287.5, scale=-1.0)
-        act(R("him"), R("hsg"), F.Relu)
-        scan(R("zs", 416, 832), R("r32"), R("zt", 416, 832), 0.0, A.mult, A.min)
-        if first:
-            ts(R("lp", 1, 2), R("tint", 7, 8), 4.0, A.mult, col(CA8), A.add)
-        else:
-            send_p()
-        copy(R("zw", 0, 26), R("zs", 31, 832, 32))
-        copy(R("zw", 32, 58), R("zs", 31, 832, 32))
+        turn(R("zt", 0, 416), R("cum", 0, 416))
+        turn(R("zt", 416, 832), R("cum", 416, 832))
+        scan(R("zs", 0, 416), R("r32"), R("zt", 0, 416), 0.0, A.max, A.min)
+        scan(R("zs", 416, 832), R("r32"), R("zt", 416, 832), 0.0, A.max, A.min)
         if first:
             ts(R("tint", 8, 9), p0, 3, A.logical_shift_right, 2, A.bitwise_and)
-        turn(R("zu"), R("zw", 0, 64))
-        if first:
-            tt(R("tint", 9, 10), R("tint", 8, 9), R("pint", 4, 5), A.add)
-        turn(R("zw", 64, 96), R("zu", 16, 48))
-        if first:
-            ts(R("tint", 10, 11), R("tint", 9, 10), 15, A.bitwise_and)
-        ts(R("lpos"), (R("zw"), R("lp")), 1406.0, A.add, 0.5, A.mult)
-        if first:
-            send_p()
+            ts(R("tint", 5, 6), p0, 15, A.bitwise_and, 1, A.logical_shift_right)
+        else:
+            quant(pq, pp, p, 0, 128)
+        ts(R("lpos", 0, 26), R("zs", 31, 832, 32), 1406.0, A.add, 0.5, A.mult)
         ends = R("lpos", 24, 26)
+        cut = 128 if first else 256
+        quant(pq, pp, p, cut - 128, cut)
+        send(nq, pq, "gotp%d" % t, 0, cut, codes=True)
         copy((R("srt"), R("lpos", 0, 24)), R("key"))
-        if first:
-            copy(col(CSH), R("tint", 10, 11))
+        quant(pq, pp, p, cut, C)
+        send(nq, pq, "gotp%d" % t, cut, C, codes=True)
+        send(npl, pp, "gotp%d" % t)
         scan(R("ymin", 1, 385), R("srt"), R("srt"), HUGE, A.min, A.min)
         if first:
-            ts(R("lsh"), R("row16"), col(CSH), A.add, col(C64), A.add)
+            tt(R("tint", 9, 10), R("tint", 8, 9), R("pint", 4, 5), A.add)
+            copy(col(CH), R("tint", 5, 6))
+            act(col(CB2), col(CH), F.Identity, bias=col(CG), scale=2.0)
+            act(col(CB3), col(CB2), F.Identity, bias=16.0)
+        else:
+            tt(R("dg", 0, 128), bank(4, 128), R("diag", 0, 128), A.mult)
         scan(R("ymin", 393, 777), R("srt"), R("ymin", 0, 384), HUGE, A.min, A.max)
+        if first:
+            ts(R("tint", 10, 11), R("tint", 9, 10), 15, A.bitwise_and)
         tt(R("firsts", 32, 64), (R("ymin", 0, 392), ends), R("crow", 0, 32), A.subtract)
-        scan(R("ymin", 785, 1169), R("srt"), R("ymin", 392, 776), HUGE, A.min, A.max)
+        if first:
+            copy(col(CSH), R("tint", 10, 11))
         tt(R("firsts", 96, 128), (R("ymin", 392, 784), ends), R("crow", 32, 64), A.subtract)
+        if first:
+            ts(R("lsh"), R("row16"), col(CSH), A.add, col(C64), A.add)
+        scan(R("ymin", 785, 1169), R("srt"), R("ymin", 392, 776), HUGE, A.min, A.max)
+        turn(R("ta", 64, 160), R("firsts", 32, 128))
         tt(R("firsts", 160, 192), (R("ymin", 784, 1176), ends), R("crow", 32, 64), A.subtract)
-        turn(R("ta", 64, 224), R("firsts", 32, 192))
-        copy(R("tb"), (R("ta"), R("lsh")))
-        for k in (1, 2, 3, 0):
-            turn(R("firsts", 64 * k, 64 * k + 32), R("tb", 32 * k, 32 * k + 32))
-        tt(R("r1"), R("firsts", 96, 130), R("firsts", 31, 65), A.max)
-        ts(R("r2"), R("firsts", 95, 129), -4096.0, A.add)
-        tt(R("r3"), R("r1"), R("firsts", 160, 194), A.min)
-        tt(R("r4"), R("r2"), R("firsts", 30, 64), A.min)
-        tt(R("vi"), R("r3"), R("r4"), A.min)
-        ts(R("vf"), R("vi"), 0xFFC007, A.bitwise_and)
-        ts(R("vn"), R("vi"), 3, A.logical_shift_right, 511, A.bitwise_and)
-        ts(R("vg"), R("vf"), 2048.0, A.mult, 18432.0, A.min)
-        tt(R("tab%d" % t), R("vg"), R("vn"), A.add)
-        send("land%d" % t, "tab%d" % t, "gott%d" % t)
+        copy(R("tb", 0, 96), (R("ta", 0, 224), R("lsh", 0, 6)))
+        turn(R("ta", 224, 256), R("firsts", 160, 192))
         if first:
             ts(R("em", 2048, 2560, 4), R("grow"), col(CGI), A.is_equal, col(CF), A.mult)
-            ts(R("diag"), R("k16"), col(CI), A.is_equal)
+        for k in (1, 2, 0):
+            turn(R("firsts", 64 * k, 64 * k + 32), R("tb", 32 * k, 32 * k + 32))
+        copy(R("tb", 96, 128), (R("ta", 224, 320), R("lsh", 0, 2)))
+        ts(R("r2"), R("firsts", 95, 129), -4096.0 * UP, A.add)
+        tt(R("r1"), R("firsts", 96, 130), R("firsts", 31, 65), A.max)
+        turn(R("firsts", 192, 224), R("tb", 96, 128))
+        tt(R("r4"), R("r2"), R("firsts", 30, 64), A.min)
+        tt(R("r3"), R("r1"), R("firsts", 160, 194), A.min)
+        if first:
             quant("eq", "es", "em", 512, 640)
             mm(4, "eq", "es", 4, "bq", "bs")
-            quant("eq", "es", "em", 0, 512)
-        tt(R("dg"), bank(4), R("diag"), A.mult)
+        tt(R("vi"), R("r3"), R("r4"), A.min)
         if first:
-            ts(R("lq", 0, 1), R("tint", 6, 7), 4.0, A.mult, col(CB2), A.add)
-        scan(R("dgs"), R("r16"), R("dg"), 0.0, A.mult, A.add)
+            ts(R("diag"), R("k16"), col(CI), A.is_equal)
+        ts(R("vf"), R("vi"), 0x7E003800, A.bitwise_and)
+        ts(R("vn"), R("vi"), 14, A.logical_shift_right, 511, A.bitwise_and)
         if first:
-            ts(R("lq", 1, 2), R("tint", 7, 8), 4.0, A.mult, col(CB3), A.add)
-            memset(R("fj", 24, 32), 0)
-            memset(R("fj", 56, 64), 0)
+            quant("eq", "es", "em", 0, 128)
+        tt(R("tab%d" % t), R("vf"), R("vn"), A.add)
+        send("land%d" % t, "tab%d" % t, "gott%d" % t)
+        lo = 0 if first else 128
+        tt(R("dg", lo, C), R("ps", 2048 + lo, 2048 + C), R("diag", lo, C), A.mult)
+        if first:
+            quant("eq", "es", "em", 128, 512)
         else:
             quant("vq", "vs", "vt")
-        ts(R("lask"), R("dgs", 15, C, 16), 33.0, A.add)
+        scan(R("dgs"), R("r16"), R("dg"), 0.0, A.mult, A.add)
+        if first:
+            ts(R("tint", 6, 8), R("pint", 2, 4), 16, A.bitwise_and)
+        ts(R("lask"), R("dgs", 15, C, 16), 143.5, A.add)
         for b in range(4):
             mm(b, "eq", "es", b, nq, npl)
         for h in range(1, 8):
             act(R("dist", 36 * h, 36 * h + 34), R("land%d" % t), F.Abs, bias=1.0 - 2048 * h)
-        ts(R("dist", 0, 34), R("land%d" % t), 1.0, A.add)
+            if h == 3:
+                ts(R("dist", 0, 34), R("land%d" % t), 1.0, A.add)
+                if first:
+                    ts(R("lq", 0, 1), R("tint", 6, 7), 4.0, A.mult, col(CB2), A.add)
+                    ts(R("lq", 1, 2), R("tint", 7, 8), 4.0, A.mult, col(CB3), A.add)
+                scan(R("ans", 0, 144), R("k512"), R("dist", 0, 144), 4096.0, A.add, A.min)
         for b in range(4):
             act(R("dwin", 392 * b + 1, 392 * b + 385), bank(b), F.Copy)
-        scan(R("ans"), R("k512"), R("dist"), 4096.0, A.add, A.min)
+        if first:
+            memset(R("fj", 24, 32), 0)
+        scan(R("ans", 144, 288), R("k512"), R("dist", 144, 288), 4096.0, A.add, A.min)
+        if first:
+            memset(R("fj", 56, 64), 0)
         for lo, hi in SPANS:
-            tt(R("z2", lo, hi), (R("ans"), R("lask", lo // 16, hi // 16)), R("him", lo, hi), A.mult)
+            tt(R("z2", lo, hi), (R("ans"), R("lask", lo // 16, hi // 16)), R("him", lo, hi), A.min)
         for lo, hi in SPANS:
             turn(R("zt2", lo, hi), R("z2", lo, hi))
         for lo, hi in SPANS:
@@ -478,10 +495,10 @@ def rank_program(g, core, T, topo):
         nx = "x%d" % (t + 1)
         for k, (lo, hi) in enumerate(SPANS):
             found = R("lfound", lo // 16, hi // 16)
-            for b in range(2 - k, 4):
-                act(R("mg", C * (b - 1) + lo, C * (b - 1) + hi), (R("dwin", 392 * b, 392 * b + 392), found), F.Copy)
+            for b in range(2 - 2 * k, 4):
+                act(R("mg", C * b + lo, C * b + hi), (R("dwin", 392 * b, 392 * b + 392), found), F.Copy)
             for b in range(4):
-                src = (R("dwin", 392 * b, 392 * b + 392), found) if b < 2 - k else R("mg", C * (b - 1) + lo, C * (b - 1) + hi)
+                src = (R("dwin", 392 * b, 392 * b + 392), found) if b < 2 - 2 * k else R("mg", C * b + lo, C * b + hi)
                 tt(R(nx, 4 * lo + b, 4 * hi, 4), src, R(p, 4 * lo + b, 4 * hi, 4), A.add)
                 if k == 1 and b == 0:
                     quant("xq%d" % (t + 1), "xs%d" % (t + 1), nx, *SPANS[0])
@@ -498,5 +515,5 @@ def rank_program(g, core, T, topo):
                 dma("sa"[m % 2], lambda m=m: T.osc[4 * m:4 * m + 4, :], lambda m=m: T[xs][32 * m:32 * m + 4, :], [R(xs)], [outs[4 + m]])
         act(R("yb", lo, hi), bank(5 + k, hi - lo), F.Copy)
         dma("a", lambda lo=lo, hi=hi: T.y[:, lo:hi], lambda lo=lo, hi=hi: T.yb[:, lo:hi], [R("yb", lo, hi)], [outs[2 + k]])
-    add("g", lambda: g.wait_ge(T.sem.sent, 3 * ROUNDS * lanes_out), outs, [], "end")
+    add("g", lambda: g.wait_ge(T.sem.sent, 4 * ROUNDS * lanes_out), outs, [], "end")
     emit(g, T, ops)

@@ -20,11 +20,11 @@ SCRATCH = {
     "ps": ("psum", [128, 4096], "float32"),
     "ut": sb(512, "bfloat16"), "vt": sb(512, "bfloat16"), "uq": sb(128, X4), "us": sb(128, "uint8"),
     "vq": sb(128, X4), "vs": sb(128, "uint8"), "wq": sb(512, X4), "wp": sb(512, "uint8"),
-    "fm": sb(2560, "bfloat16"), "fq": sb(640, X4), "fs": sb(640, "uint8"),
+    "fm": sb(1024, "bfloat16"), "fq": sb(640, X4), "fs": sb(640, "uint8"),
     "em": sb(2560, "bfloat16"), "eq": sb(640, X4), "es": sb(640, "uint8"),
     "pint": sb(8, "int32"), "tint": sb(12, "int32"), "col": sb(24, "float32"),
     "krow": sb(48, "float32"), "eqm": sb(48, "float32"), "mul": sb(48, "float32"), "pw": sb(48, "float32"),
-    "vrow": sb(64, "float32"), "vb": sb(64, "int32"), "vc": sb(64, "int32"), "sg": sb(64, "bfloat16"),
+    "vrow": sb(64, "float32"), "vb": sb(64, "int32"), "vc": sb(64, "int32"), "sg": sb(64, "bfloat16"), "near": sb(32, "float32"),
     "qrow": sb(128, "bfloat16"), "grow": sb(128, "bfloat16"), "wmask": sb(32, "bfloat16"), "w32": sb(32, "bfloat16"),
     "ones": sb(128, "bfloat16"), "ident": sb(128, "bfloat16"),
     "wcon": sb(C, "float32"), "k16": sb(C, "bfloat16"), "diag": sb(C, "bfloat16"),
@@ -38,7 +38,7 @@ SCRATCH = {
     "r1": sb(34, "float32"), "r2": sb(34, "float32"), "r3": sb(34, "float32"), "r4": sb(34, "float32"),
     "vi": sb(34, "int32"), "vf": sb(34, "int32"), "vn": sb(34, "int32"),
     "him": sb(C, "bfloat16"), "dg": sb(C, H16), "dgs": sb(C, H16), "lask": sb(24, "uint16"),
-    "dist": sb(288, "float32"), "ans": sb(288, "float32"),
+    "dist": sb(288, "float32"), "ans": sb(288, "float32"), "zg": sb(C, H16),
     "z2": sb(C, H16), "zt2": sb(C, H16), "zs2": sb(C, H16), "fi": sb(24, "int32"), "fj": sb(96, "int32"), "fu": sb(64, "int32"),
     "lfound": sb(32, "uint16"), "dwin": sb(4 * 392, "float32"), "mg": sb(4 * C, "bfloat16"), "yb": sb(C, "float32"),
 }
@@ -59,7 +59,7 @@ NPOOL = 120
 SEMAPHORES = ["s%d" % _i for _i in range(NPOOL)] + ["sent"] + ["gotp%d" % _t for _t in range(ROUNDS)] + ["gott%d" % _t for _t in range(ROUNDS)]
 
 CI, CL, CG, CGI, CQ, CB2, CB3, C31, CB, CEQ, CW, CNL, CF, CSH, CO, CE, C64, CH = range(18)
-WLO, WF, W9, PSH = 15, 6, 31, 40
+WLO, WF, W9, PSH = 15, 6, 31, 47
 
 
 def meet(r, s):
@@ -190,9 +190,10 @@ def rank_program(g, core, T, topo):
     def turn(o, i):
         add("v", lambda: V.transpose(ap(o), ap(i)), [i], [o])
 
-    def quant(c, s, i, lo=0, hi=None):
+    def quant(c, s, i, lo=0, hi=None, at=None):
         hi = SCRATCH[c][1][1] if hi is None else hi
-        a, b, d = R(c, lo, hi), R(s, lo, hi), R(i, 4 * lo, 4 * hi)
+        at = lo if at is None else at
+        a, b, d = R(c, lo, hi), R(s, lo, hi), R(i, 4 * at, 4 * (at + hi - lo))
         add("v", lambda: V.quantize_mx(ap(a), ap(b), ap(d)), [d], [a, b])
 
     def act(o, i, func, bias=None, scale=None, acc=None):
@@ -252,68 +253,69 @@ def rank_program(g, core, T, topo):
         arrive("gott%d" % t, lanes_in, ["land%d" % t])
 
     iota(R("pint", 0, 1), [[0, 1]], 0, 1)
-    iota(R("krow", 0, 32), [[0, 2], [-1, 16]], 15, 0)
-    iota(R("krow", 32, 48), [[1, 16]], 0, 0)
-    iota(R("vrow", 0, 32), [[-1, 32]], 31, 0)
-    iota(R("vrow", 32, 64), [[0, 2], [32, 16]], 0, 0)
+    iota(R("krow"), [[0, 3], [-1, 16]], 15, 0)
+    iota(R("vrow", 0, 32), [[-256, 32]], 31 * 256, 0)
+    iota(R("vrow", 32, 64), [[0, 2], [8192, 16]], 0, 0)
     iota(R("qrow"), [[1, 4], [0, 32]], 0, 0)
     iota(R("grow"), [[1, 8], [0, 16]], 0, 0)
-    iota(R("wcon"), [[8 * int(UP), C]], 0, 0)
-    iota(R("r32"), [[0, 13], [-2048, 32]], 0, 0)
     iota(R("pint", 2, 4), [[0, 2]], 0, 17)
     iota(R("pint", 4, 5), [[0, 1]], 15, 1)
+    iota(R("wcon"), [[8 * int(UP), C]], 0, 0)
+    iota(R("r32"), [[0, 13], [-2048, 32]], 0, 0)
     iota(R("row16"), [[64, 4], [16, 2]], 0, 0)
     iota(R("k16"), [[0, 24], [1, 16]], 0, 0)
-    memset(R("fm", 0, 1024), 0.0)
-    act(R("fm", 1024, 2048), R("fm", 0, 1024), F.Copy)
-    act(R("fm", 2048, 2560), R("fm", 1024, 1536), F.Copy)
-    act(R("bits", 0, 768), R("fm", 1024, 1792), F.Copy)
-    memset(R("mul"), 2.0)
     p0 = R("pint", 0, 1)
+    memset(R("fm", 0, 512), 0.0)
+    for b in range(1, 4):
+        act(R("bits", b, 4 * C, 4), R("fm", 0, C), F.Copy)
+    memset(R("mul"), 2.0)
     ts(R("tint", CI, CI + 1), p0, 15, A.bitwise_and)
-    ts(R("tint", CL, CL + 1), p0, 31, A.bitwise_and)
-    memset(R("mul", 16, 27), 1.0)
     ts(R("tint", CG, CG + 1), p0, 4, A.logical_shift_right, 1, A.bitwise_and)
-    ts(R("tint", CGI, CGI + 1), p0, 4, A.logical_shift_right)
+    memset(R("mul", 16, 27), 1.0)
+    memset(R("mul", 33, 48), 0.5)
     ts(R("tint", CQ, CQ + 1), p0, 5, A.logical_shift_right)
+    ts(R("tint", CL, CL + 1), p0, 31, A.bitwise_and)
+    ts(R("tint", CGI, CGI + 1), p0, 4, A.logical_shift_right)
     memset(R("mul", 4, 12, 7), 0.0)
     memset(R("mul", 23, 33, 9), 0.0)
     copy(R("col", 0, 5), R("tint", 0, 5))
-    memset(R("a0", 0, 1), 0.0)
-    memset(R("a1", 0, 1), 0.0)
+    memset(R("fm", 512, 768), 0.0)
     ts(R("eqm"), R("krow"), col(CI), A.is_equal)
-    ts(col(C31), col(CL), -1.0, A.mult, 31.0, A.add)
-    memset(R("ones"), 1.0)
+    memset(R("fm", 768, 1024), 0.0)
     scan(R("pw"), R("mul"), R("eqm"), 0.0, A.mult, A.add)
-    ts(R("b0", 384, 416), R("vrow", 0, 32), col(C31), A.is_equal, 1022.0, A.mult)
-    ts(R("b1", 384, 416), R("vrow", 0, 32), col(C31), A.is_equal, 1022.0, A.mult)
+    ts(R("tint", 8, 9), p0, 3, A.logical_shift_right, 2, A.bitwise_and)
+    ts(R("tint", 5, 6), p0, 15, A.bitwise_and, 1, A.logical_shift_right)
     ts(col(CO), pw(WLO), col(CG), A.mult)
     ts(R("vb"), R("vrow"), pw(PSH), A.mult)
-    ts(col(CW), pw(WF), -UP / 2, A.mult)
-    ts(col(CE), col(CO), -1.0, A.mult, pw(WLO), A.add)
+    ts(col(CE), pw(WLO), col(CO), A.subtract)
     ts(R("vc"), R("vb"), 256, A.bitwise_and)
     ts(R("fm", 512, 1024, 4), R("qrow"), col(CQ), A.is_equal, col(CO), A.mult)
-    ts(R("wmask"), R("grow", 0, 32), col(CG), A.is_equal, pw(W9), A.mult)
-    ts(R("sg", 32, 64), R("vc", 32, 64), 64 * UP, A.mult, -8192 * UP, A.add)
-    ts(R("sg", 0, 32), R("vc", 0, 32), -1.0 / 128, A.mult, 1.0, A.add)
     ts(R("fm", 0, 512, 4), R("qrow"), col(CQ), A.is_equal, col(CE), A.mult)
+    ts(R("sg", 0, 32), R("vc", 0, 32), -1.0 / 128, A.mult, 1.0, A.add)
+    ts(R("sg", 32, 64), R("vc", 32, 64), 64 * UP, A.mult, -8192 * UP, A.add)
+    ts(R("wmask"), R("grow", 0, 32), col(CG), A.is_equal, pw(W9), A.mult)
+    quant("fq", "fs", "fm", 0, 256)
     tt(R("w32"), R("sg", 32, 64), R("wmask"), A.mult)
-    ts(R("fm", 2048, 2560, 4), R("grow"), col(CGI), A.is_equal, col(CW), A.mult)
+    act(col(C31), col(CL), F.Identity, bias=31.0, scale=-1.0)
+    act(col(CEQ), col(CL), F.Identity, bias=-31.0, scale=2.0)
+    act(col(CB), col(CL), F.Identity, bias=-32.0, scale=2.0)
+    act(R("near"), R("vrow", 0, 32), F.Abs, bias=col(C31), scale=-1.0 / 256)
+    act(col(CW), pw(WF), F.Copy, scale=-UP / 2)
+    act(R("ones"), R("qrow"), F.Identity, bias=1.0, scale=0.0)
+    add("g", lambda: g.affine_select(T.ident[:], T.ones[:], [[-1, 128]], A.is_equal, 0.0, 0, 1), [R("ones")], [R("ident")])
+    for k in range(2):
+        act(R("a%d" % k, 0, 1), col(CL), F.Copy, scale=0.0)
+        act(R("a%d" % k, 385, 416), R("near", 0, 31), F.Relu, bias=1024.0, scale=-1024.0)
+        act(R("b%d" % k, 384, 416), R("near"), F.Relu, bias=1022.0, scale=-1022.0)
     for lo in range(0, 128, 32):
         hi = lo + 32
-        add("a", lambda lo=lo, hi=hi: S.activation(T.fm[lo:hi, 1024 + 4 * lo:1024 + 4 * hi:4], T.sg[lo:hi, 0:32], F.Identity, scale=T.col[lo:hi, CO:CO + 1]),
-            [R("sg", 0, 32), col(CO)], [R("fm", 1024 + 4 * lo, 1024 + 4 * hi, 4)])
-        add("a", lambda lo=lo, hi=hi: S.activation(T.fm[lo:hi, 1536 + 4 * lo:1536 + 4 * hi:4], T.w32[lo:hi, :], F.Copy),
-            [R("w32")], [R("fm", 1536 + 4 * lo, 1536 + 4 * hi, 4)])
-    act(R("a0", 385, 416), R("vrow", 0, 31), F.Abs, bias=col(C31), scale=-1.0)
-    act(col(CB), col(CL), F.Identity, bias=-32.0, scale=2.0)
-    act(col(CEQ), col(CL), F.Identity, bias=-31.0, scale=2.0)
-    act(R("a1", 385, 416), R("a0", 385, 416), F.Relu, bias=1024.0, scale=-1024.0)
-    add("g", lambda: g.affine_select(T.ident[:], T.ones[:], [[-1, 128]], A.is_equal, 0.0, 0, 1), [R("ones")], [R("ident")])
-    memset(R("bits", 768, 1536), 0.0)
-    quant("fq", "fs", "fm", 0, 256)
+        add("a", lambda lo=lo, hi=hi: S.activation(T.fm[lo:hi, 4 * lo:4 * hi:4], T.sg[lo:hi, 0:32], F.Identity, scale=T.col[lo:hi, CO:CO + 1]),
+            [R("sg", 0, 32), col(CO)], [R("fm", 4 * lo, 4 * hi, 4)])
+    for lo in range(0, 128, 32):
+        hi = lo + 32
+        add("a", lambda lo=lo, hi=hi: S.activation(T.fm[lo:hi, 512 + 4 * lo:512 + 4 * hi:4], T.w32[lo:hi, :], F.Copy),
+            [R("w32")], [R("fm", 512 + 4 * lo, 512 + 4 * hi, 4)])
     quant("uq", "us", "ut")
-
     quant("xq0", "xs0", "x0", *SPANS[0])
     for t in range(ROUNDS):
         x, xq, xs = "x%d" % t, "xq%d" % t, "xs%d" % t
@@ -334,24 +336,30 @@ def rank_program(g, core, T, topo):
         for k, (lo, hi) in enumerate(SPANS):
             act(R("bits", 4 * lo, 4 * hi, 4), bank(4 + k, hi - lo), F.Sign, bias=TINY)
         if first:
-            act(R("a0", 385, 416), R("a1", 385, 416), F.Copy)
-            quant("fq", "fs", "fm", 256, 640)
+            quant("fq", "fs", "fm", 256, 512, 0)
+            tt(R("tint", 9, 10), R("tint", 8, 9), R("pint", 4, 5), A.add)
         else:
             layer(0)
         quant("bq", "bs", "bits", *s0)
         mm(2, "fq", "fs", 0, "bq", "bs", *s0)
         mm(6, "fq", "fs", 2, "bq", "bs", *s0)
+        if first:
+            ts(R("fm", 0, 512, 4), R("grow"), col(CGI), A.is_equal, col(CW), A.mult)
         quant("bq", "bs", "bits", *s1)
         mm(3, "fq", "fs", 0, "bq", "bs", *s1)
-        mm(4, "fq", "fs", 0, "bq", "bs")
         mm(1, "fq", "fs", 2, "bq", "bs", *s1)
+        mm(4, "fq", "fs", 0, "bq", "bs")
         mm(5, "fq", "fs", 1, "bq", "bs")
+        if first:
+            quant("fq", "fs", "fm", 512, 640, 0)
         mm(7, "fq", "fs", 3, "bq", "bs", tiles=2)
         ts(R("a0", 1, 1 + s0[1]), bank(2, s0[1]), col(CEQ), A.is_equal, 1024.0, A.mult)
         act(R("a1", 1, 1 + s0[1]), bank(6, s0[1]), F.Relu, bias=-512.0 * 29, scale=512.0)
         act(R("junk", 0, C), bank(4), F.Sign, bias=col(CB), scale=-1.0, acc=R("base", 0, 1))
         act(R("junk", C, 2 * C), bank(5), F.Sign, bias=col(CB), scale=-1.0, acc=R("base", 1, 2))
         ts(R("a0", 1 + s1[0], 1 + C), bank(3, C - s1[0]), col(CEQ), A.is_equal, 1024.0, A.mult)
+        if first:
+            ts(R("tint", 10, 11), R("tint", 9, 10), 15, A.bitwise_and)
         ts(R("a1", 1 + s1[0], 1 + C), bank(1, C - s1[0]), 31.0, A.is_equal, 1024.0, A.mult)
         ts(R("b0", 0, C), R("a0", 1, 1 + C), 1022.0 / 1024, A.mult)
         ts(R("b1", 0, C), R("a1", 1, 1 + C), 1022.0 / 1024, A.mult)
@@ -359,20 +367,17 @@ def rank_program(g, core, T, topo):
             layer(b)
         if not first:
             mm(4, "eq", "es", 4, "bq", "bs")
-        scan(R("cnt", 0, 416), R("a0"), R("b0"), R("base", 0, 1), A.add, A.subtract)
-        key(0, 128)
-        copy(R("cum", 0, 832, 2), R("cnt", 0, 416))
-        scan(R("cnt", 416, 832), R("a1"), R("b1"), R("base", 1, 2), A.add, A.subtract)
-        key(128, 256)
-        copy(R("cum", 1, 832, 2), R("cnt", 416, 832))
-        key(256, C)
-        act(R("him"), R("key"), F.Relu, bias=MISS - MID, scale=-1.0 / UP)
+        scan(R("cnt", 0, 416), R("a0"), R("b0"), 0.0, A.add, A.subtract)
+        scan(R("cnt", 416, 832), R("a1"), R("b1"), 0.0, A.add, A.subtract)
+        ts(R("cum", 0, 832, 2), R("cnt", 0, 416), R("base", 0, 1), A.add)
+        ts(R("cum", 1, 832, 2), R("cnt", 416, 832), R("base", 1, 2), A.add)
+        key(0, 192)
         if first:
             fill(R("ymin", 0, 3 * 392, 392), HUGE)
             for k in range(3):
                 fill(R("ymin", 392 * k + 385, 392 * k + 392), HUGE)
-            act(R("crow", 0, 32), R("vrow", 0, 32), F.Identity, bias=-UP * MID, scale=16384 * UP)
-            act(R("crow", 32, 64), R("vrow", 0, 32), F.Identity, bias=-UP * (MID + 8192), scale=16384 * UP)
+            act(R("crow", 0, 32), R("vrow", 0, 32), F.Identity, bias=-UP * MID, scale=64 * UP)
+            act(R("crow", 32, 64), R("vrow", 0, 32), F.Identity, bias=-UP * (MID + 8192), scale=64 * UP)
             act(col(C64), col(CG), F.Copy, scale=64.0)
             fill(R("firsts", 64, 96), 0.0)
             fill(R("ta", 0, 64), 0.0)
@@ -381,7 +386,8 @@ def rank_program(g, core, T, topo):
             act(col(CNL), pw(WLO), F.Copy, scale=0.5)
             act(R("em", 2048, 2560), R("fm", 0, 512), F.Copy, scale=0.0)
             act(col(CF), pw(WF), F.Identity, bias=col(CNL), scale=-18.0)
-            act(R("em", 0, 2048), R("fm", 0, 2048), F.Copy, scale=0.0)
+            for lo in (0, 1024):
+                act(R("em", lo, lo + 1024), R("fm"), F.Copy, scale=0.0)
             act(R("r16"), R("k16"), F.Sign)
             for b in range(4):
                 act(R("em", 512 * b + b, 512 * b + 512, 4), R("ident"), F.Copy)
@@ -395,34 +401,22 @@ def rank_program(g, core, T, topo):
         turn(R("zt", 416, 832), R("cum", 416, 832))
         scan(R("zs", 0, 416), R("r32"), R("zt", 0, 416), 0.0, A.max, A.min)
         scan(R("zs", 416, 832), R("r32"), R("zt", 416, 832), 0.0, A.max, A.min)
-        if first:
-            ts(R("tint", 8, 9), p0, 3, A.logical_shift_right, 2, A.bitwise_and)
-            ts(R("tint", 5, 6), p0, 15, A.bitwise_and, 1, A.logical_shift_right)
-        else:
-            quant(pq, pp, p, 0, 128)
+        key(192, C)
+        act(R("him"), R("key"), F.Relu, bias=MISS - MID, scale=-1.0 / UP)
         ts(R("lpos", 0, 26), R("zs", 31, 832, 32), 1406.0, A.add, 0.5, A.mult)
         ends = R("lpos", 24, 26)
-        cut = 128 if first else 256
-        quant(pq, pp, p, cut - 128, cut)
-        send(nq, pq, "gotp%d" % t, 0, cut, codes=True)
+        quant(pq, pp, p, 0, 128)
+        send(nq, pq, "gotp%d" % t, 0, 128, codes=True)
         copy((R("srt"), R("lpos", 0, 24)), R("key"))
-        quant(pq, pp, p, cut, C)
-        send(nq, pq, "gotp%d" % t, cut, C, codes=True)
-        send(npl, pp, "gotp%d" % t)
+        quant(pq, pp, p, 128, 256)
         scan(R("ymin", 1, 385), R("srt"), R("srt"), HUGE, A.min, A.min)
-        if first:
-            tt(R("tint", 9, 10), R("tint", 8, 9), R("pint", 4, 5), A.add)
-            copy(col(CH), R("tint", 5, 6))
-            act(col(CB2), col(CH), F.Identity, bias=col(CG), scale=2.0)
-            act(col(CB3), col(CB2), F.Identity, bias=16.0)
-        else:
-            tt(R("dg", 0, 128), bank(4, 128), R("diag", 0, 128), A.mult)
+        quant(pq, pp, p, 256, C)
+        send(nq, pq, "gotp%d" % t, 128, C, codes=True)
+        send(npl, pp, "gotp%d" % t)
         scan(R("ymin", 393, 777), R("srt"), R("ymin", 0, 384), HUGE, A.min, A.max)
         if first:
-            ts(R("tint", 10, 11), R("tint", 9, 10), 15, A.bitwise_and)
-        tt(R("firsts", 32, 64), (R("ymin", 0, 392), ends), R("crow", 0, 32), A.subtract)
-        if first:
             copy(col(CSH), R("tint", 10, 11))
+        tt(R("firsts", 32, 64), (R("ymin", 0, 392), ends), R("crow", 0, 32), A.subtract)
         tt(R("firsts", 96, 128), (R("ymin", 392, 784), ends), R("crow", 32, 64), A.subtract)
         if first:
             ts(R("lsh"), R("row16"), col(CSH), A.add, col(C64), A.add)
@@ -453,15 +447,17 @@ def rank_program(g, core, T, topo):
             quant("eq", "es", "em", 0, 128)
         tt(R("tab%d" % t), R("vf"), R("vn"), A.add)
         send("land%d" % t, "tab%d" % t, "gott%d" % t)
-        lo = 0 if first else 128
-        tt(R("dg", lo, C), R("ps", 2048 + lo, 2048 + C), R("diag", lo, C), A.mult)
+        if first:
+            copy(col(CH), R("tint", 5, 6))
+            ts(R("tint", 6, 8), R("pint", 2, 4), 16, A.bitwise_and)
+            act(col(CB2), col(CH), F.Identity, bias=col(CG), scale=2.0)
+            act(col(CB3), col(CB2), F.Identity, bias=16.0)
+        tt(R("dg"), bank(4), R("diag"), A.mult)
         if first:
             quant("eq", "es", "em", 128, 512)
         else:
             quant("vq", "vs", "vt")
         scan(R("dgs"), R("r16"), R("dg"), 0.0, A.mult, A.add)
-        if first:
-            ts(R("tint", 6, 8), R("pint", 2, 4), 16, A.bitwise_and)
         ts(R("lask"), R("dgs", 15, C, 16), 143.5, A.add)
         for b in range(4):
             mm(b, "eq", "es", b, nq, npl)
@@ -473,15 +469,16 @@ def rank_program(g, core, T, topo):
                     ts(R("lq", 0, 1), R("tint", 6, 7), 4.0, A.mult, col(CB2), A.add)
                     ts(R("lq", 1, 2), R("tint", 7, 8), 4.0, A.mult, col(CB3), A.add)
                 scan(R("ans", 0, 144), R("k512"), R("dist", 0, 144), 4096.0, A.add, A.min)
-        for b in range(4):
-            act(R("dwin", 392 * b + 1, 392 * b + 385), bank(b), F.Copy)
         if first:
             memset(R("fj", 24, 32), 0)
         scan(R("ans", 144, 288), R("k512"), R("dist", 144, 288), 4096.0, A.add, A.min)
         if first:
             memset(R("fj", 56, 64), 0)
-        for lo, hi in SPANS:
-            tt(R("z2", lo, hi), (R("ans"), R("lask", lo // 16, hi // 16)), R("him", lo, hi), A.min)
+        tt(R("z2", *s0), (R("ans"), R("lask", 0, s0[1] // 16)), R("him", *s0), A.min)
+        act(R("zg", *s1), (R("ans"), R("lask", s1[0] // 16, C // 16)), F.Copy)
+        for b in range(4):
+            act(R("dwin", 392 * b + 1, 392 * b + 385), bank(b), F.Copy)
+        tt(R("z2", *s1), R("zg", *s1), R("him", *s1), A.min)
         for lo, hi in SPANS:
             turn(R("zt2", lo, hi), R("z2", lo, hi))
         for lo, hi in SPANS:

@@ -10,6 +10,7 @@ MISS = 524288.0
 MID = 8192.0 * 31 + 2 * MISS + 3.5
 HUGE = UP * (MISS - MID)
 TINY = 1e-37
+ASK = C + 16
 
 
 def sb(n, dtype):
@@ -21,25 +22,25 @@ SCRATCH = {
     "ut": sb(512, "bfloat16"), "vt": sb(512, "bfloat16"), "uq": sb(128, X4), "us": sb(128, "uint8"),
     "vq": sb(128, X4), "vs": sb(128, "uint8"), "wq": sb(512, X4), "wp": sb(512, "uint8"),
     "fm": sb(1024, "bfloat16"), "fq": sb(640, X4), "fs": sb(640, "uint8"),
-    "em": sb(2560, "bfloat16"), "eq": sb(640, X4), "es": sb(640, "uint8"),
-    "pint": sb(8, "int32"), "tint": sb(12, "int32"), "col": sb(24, "float32"),
+    "em": sb(1536, "bfloat16"), "eq": sb(640, X4), "es": sb(640, "uint8"),
+    "pint": sb(8, "int32"), "tint": sb(12, "int32"), "col": sb(32, "float32"),
     "krow": sb(48, "float32"), "eqm": sb(48, "float32"), "mul": sb(48, "float32"), "pw": sb(48, "float32"),
     "vrow": sb(64, "float32"), "vb": sb(64, "int32"), "vc": sb(64, "int32"), "sg": sb(64, "bfloat16"), "near": sb(32, "float32"),
     "qrow": sb(128, "bfloat16"), "grow": sb(128, "bfloat16"), "wmask": sb(32, "bfloat16"), "w32": sb(32, "bfloat16"),
-    "ones": sb(128, "bfloat16"), "ident": sb(128, "bfloat16"),
+    "qe": sb(128, "bfloat16"), "qo": sb(128, "bfloat16"), "ones": sb(128, "bfloat16"), "ident": sb(128, "bfloat16"),
     "wcon": sb(C, "float32"), "k16": sb(C, "bfloat16"), "diag": sb(C, "bfloat16"),
-    "r32": sb(416, "bfloat16"), "r16": sb(C, "bfloat16"), "k512": sb(144, "bfloat16"),
-    "crow": sb(64, "float32"), "row16": sb(8, "float32"), "lq": sb(2, "uint16"), "lsh": sb(8, "uint16"),
+    "r32": sb(416, "bfloat16"), "r16": sb(C, "bfloat16"), "m32": sb(C, "bfloat16"), "k512": sb(288, "bfloat16"),
+    "crow": sb(64, "float32"), "hrow": sb(8, "float32"), "hb": sb(8, "float32"), "lq": sb(2, "uint16"),
     "bits": sb(4 * C, "bfloat16"), "bq": sb(C, X4), "bs": sb(C, "uint8"),
     "a0": sb(416, "bfloat16"), "a1": sb(416, "bfloat16"), "b0": sb(416, H16), "b1": sb(416, H16),
     "cnt": sb(832, H16), "cum": ("sbuf", [128, 26, 32], H16), "base": sb(2, "float32"), "junk": sb(2 * C, "bfloat16"),
     "key": sb(C, "float32"), "srt": sb(C, "float32"), "zt": sb(832, H16), "zs": sb(832, H16), "lpos": sb(32, "uint16"),
-    "ymin": sb(3 * 392, "float32"), "firsts": sb(224, "float32"), "ta": sb(320, "float32"), "tb": sb(128, "float32"),
+    "ymin": sb(3 * 392, "float32"), "firsts": sb(256, "float32"), "ta": ("sbuf", [128, 6, 32], "float32"),
     "r1": sb(34, "float32"), "r2": sb(34, "float32"), "r3": sb(34, "float32"), "r4": sb(34, "float32"),
     "vi": sb(34, "int32"), "vf": sb(34, "int32"), "vn": sb(34, "int32"),
-    "him": sb(C, "bfloat16"), "dg": sb(C, H16), "dgs": sb(C, H16), "lask": sb(24, "uint16"),
-    "dist": sb(288, "float32"), "ans": sb(288, "float32"), "zg": sb(C, H16),
-    "z2": sb(C, H16), "zt2": sb(C, H16), "zs2": sb(C, H16), "fi": sb(24, "int32"), "fj": sb(96, "int32"), "fu": sb(64, "int32"),
+    "him": sb(ASK, "bfloat16"), "cap": sb(ASK, H16), "dg": sb(C, H16), "dgs": sb(C, H16), "lask": sb(26, "uint16"),
+    "dist": sb(288, "float32"), "ans": sb(288, "float32"), "zg": sb(ASK, H16),
+    "z2": sb(ASK, H16), "zt2": sb(2 * C, H16), "zs2": sb(2 * C, H16), "fi": sb(24, "int32"), "fj": sb(32, "int32"),
     "lfound": sb(32, "uint16"), "dwin": sb(4 * 392, "float32"), "mg": sb(4 * C, "bfloat16"), "yb": sb(C, "float32"),
 }
 for _t in range(ROUNDS + 1):
@@ -58,7 +59,7 @@ for _t in range(ROUNDS):
 NPOOL = 120
 SEMAPHORES = ["s%d" % _i for _i in range(NPOOL)] + ["sent"] + ["gotp%d" % _t for _t in range(ROUNDS)] + ["gott%d" % _t for _t in range(ROUNDS)]
 
-CI, CL, CG, CGI, CQ, CB2, CB3, C31, CB, CEQ, CW, CNL, CF, CSH, CO, CE, C64, CH = range(18)
+CI, CL, CG, CGI, CQ, CB2, CB3, C31, CB, CEQ, CW, CNL, CF, CO, CH, CX, CD, CU, CK, CT, CP, CN, CZ = range(23)
 WLO, WF, W9, PSH = 15, 6, 31, 47
 
 
@@ -154,6 +155,10 @@ def rank_program(g, core, T, topo):
             return ap(r[0]).indirect(ap(r[1]))
         if r[0] == "cum":
             return T.cum[:, :, 16 * r[1]:16 * r[1] + 16] if r[3] == 2 else T.cum[:, r[1] // 32:r[2] // 32, :]
+        if r[0] == "ta":
+            k = r[1] // 64
+            c = 16 * (r[1] % 64) if r[3] == 2 else (15 if r[2] % 64 else 1)
+            return T.ta[:, 2 * k:2 * k + 2, c:c + 16]
         return T[r[0]][:, r[1]:r[2]:r[3]] if r[3] > 1 else T[r[0]][:, r[1]:r[2]]
 
     def runs(*rs):
@@ -206,8 +211,8 @@ def rank_program(g, core, T, topo):
             kw["accum_out"] = acc
         add("a", lambda: S.activation(ap(o), ap(i), func, **{k: ap(w) for k, w in kw.items()}), runs(i, bias, scale), runs(o, acc))
 
-    def fill(o, c):
-        act(o, R("r32", 0, len(range(o[1], o[2], o[3]))), F.Identity, bias=c, scale=0.0)
+    def fill(o, c, src="r32"):
+        act(o, R(src, 0, len(range(o[1], o[2], o[3]))), F.Identity, bias=c, scale=0.0)
 
     def mm(k, lq, ls, at, rq, rs, lo=0, hi=C, tiles=1):
         o = bank(k, hi - lo)
@@ -241,6 +246,13 @@ def rank_program(g, core, T, topo):
     def arrive(sem, count, bufs):
         add("g", (sem, count), [], [R(b) for b in bufs], "arrive")
 
+    def blocks(at, src, scale):
+        for lo in range(0, 128, 32):
+            hi = lo + 32
+            kw = {"scale": T.col[lo:hi, scale:scale + 1]} if scale is not None else {}
+            add("a", lambda lo=lo, hi=hi, kw=kw: S.activation(T.fm[lo:hi, at + 4 * lo:at + 4 * hi:4], T[src][lo:hi, 0:32], F.Identity, **kw),
+                [R(src, 0, 32)] + ([col(scale)] if scale is not None else []), [R("fm", at + 4 * lo, at + 4 * hi, 4)])
+
     for lo, hi in SPANS:
         dma("s", lambda lo=lo, hi=hi: T.x0[:, 4 * lo:4 * hi], lambda lo=lo, hi=hi: T.x[:, 4 * lo:4 * hi], [], [R("x0", 4 * lo, 4 * hi)])
     dma("a", lambda: T.ut[:], lambda: T.u[:], [], [R("ut")])
@@ -249,53 +261,51 @@ def rank_program(g, core, T, topo):
         dma("s", lambda lo=lo: T.wq[:, lo:lo + 256].bitcast(dt.uint8), lambda lo=lo: T.wc[:, 4 * lo:4 * lo + 1024], [], [R("wq", lo, lo + 256)])
     dma("s", lambda: T.vt[:], lambda: T.v[:], [], [R("vt")])
     for t in range(ROUNDS):
-        arrive("gotp%d" % t, 3 * lanes_in, ["nq%d" % t, "np%d" % t])
+        arrive("gotp%d" % t, 4 * lanes_in, ["nq%d" % t, "np%d" % t])
         arrive("gott%d" % t, lanes_in, ["land%d" % t])
 
     iota(R("pint", 0, 1), [[0, 1]], 0, 1)
     iota(R("krow"), [[0, 3], [-1, 16]], 15, 0)
+    iota(R("qrow"), [[1, 4], [0, 32]], 0, 0)
     iota(R("vrow", 0, 32), [[-256, 32]], 31 * 256, 0)
     iota(R("vrow", 32, 64), [[0, 2], [8192, 16]], 0, 0)
-    iota(R("qrow"), [[1, 4], [0, 32]], 0, 0)
     iota(R("grow"), [[1, 8], [0, 16]], 0, 0)
-    iota(R("pint", 2, 4), [[0, 2]], 0, 17)
-    iota(R("pint", 4, 5), [[0, 1]], 15, 1)
     iota(R("wcon"), [[8 * int(UP), C]], 0, 0)
     iota(R("r32"), [[0, 13], [-2048, 32]], 0, 0)
-    iota(R("row16"), [[64, 4], [16, 2]], 0, 0)
+    iota(R("pint", 2, 3), [[0, 1]], 0, 17)
+    iota(R("hrow"), [[-2048, 8]], 1, 0)
     iota(R("k16"), [[0, 24], [1, 16]], 0, 0)
     p0 = R("pint", 0, 1)
-    memset(R("fm", 0, 512), 0.0)
+    memset(R("junk", 0, C), 0.0)
+    memset(R("fm", 0, 256), 0.0)
+    for lo, hi, step, c in ((0, 16, 1, 2.0), (16, 27, 1, 1.0), (27, 32, 1, 2.0), (33, 48, 1, 0.5), (4, 12, 7, 0.0), (23, 33, 9, 0.0)):
+        fill(R("mul", lo, hi, step), c, "junk")
     for b in range(1, 4):
-        act(R("bits", b, 4 * C, 4), R("fm", 0, C), F.Copy)
-    memset(R("mul"), 2.0)
+        act(R("bits", b, 4 * C, 4), R("junk", 0, C), F.Copy)
     ts(R("tint", CI, CI + 1), p0, 15, A.bitwise_and)
     ts(R("tint", CG, CG + 1), p0, 4, A.logical_shift_right, 1, A.bitwise_and)
-    memset(R("mul", 16, 27), 1.0)
-    memset(R("mul", 33, 48), 0.5)
     ts(R("tint", CQ, CQ + 1), p0, 5, A.logical_shift_right)
     ts(R("tint", CL, CL + 1), p0, 31, A.bitwise_and)
     ts(R("tint", CGI, CGI + 1), p0, 4, A.logical_shift_right)
-    memset(R("mul", 4, 12, 7), 0.0)
-    memset(R("mul", 23, 33, 9), 0.0)
+    memset(R("fm", 256, 640), 0.0)
     copy(R("col", 0, 5), R("tint", 0, 5))
-    memset(R("fm", 512, 768), 0.0)
+    memset(R("fm", 640, 1024), 0.0)
     ts(R("eqm"), R("krow"), col(CI), A.is_equal)
-    memset(R("fm", 768, 1024), 0.0)
+    ts(R("qo"), R("qrow"), col(CQ), A.is_equal, col(CG), A.mult)
+    ts(R("qe"), R("qrow"), col(CQ), A.is_equal)
     scan(R("pw"), R("mul"), R("eqm"), 0.0, A.mult, A.add)
-    ts(R("tint", 8, 9), p0, 3, A.logical_shift_right, 2, A.bitwise_and)
-    ts(R("tint", 5, 6), p0, 15, A.bitwise_and, 1, A.logical_shift_right)
-    ts(col(CO), pw(WLO), col(CG), A.mult)
+    tt(R("qe"), R("qe"), R("qo"), A.subtract)
     ts(R("vb"), R("vrow"), pw(PSH), A.mult)
-    ts(col(CE), pw(WLO), col(CO), A.subtract)
+    ts(R("fm", 512, 1024, 4), R("qo"), pw(WLO), A.mult)
+    ts(R("fm", 0, 512, 4), R("qe"), pw(WLO), A.mult)
     ts(R("vc"), R("vb"), 256, A.bitwise_and)
-    ts(R("fm", 512, 1024, 4), R("qrow"), col(CQ), A.is_equal, col(CO), A.mult)
-    ts(R("fm", 0, 512, 4), R("qrow"), col(CQ), A.is_equal, col(CE), A.mult)
-    ts(R("sg", 0, 32), R("vc", 0, 32), -1.0 / 128, A.mult, 1.0, A.add)
-    ts(R("sg", 32, 64), R("vc", 32, 64), 64 * UP, A.mult, -8192 * UP, A.add)
     ts(R("wmask"), R("grow", 0, 32), col(CG), A.is_equal, pw(W9), A.mult)
     quant("fq", "fs", "fm", 0, 256)
+    ts(R("sg", 0, 32), R("vc", 0, 32), -1.0 / 128, A.mult, 1.0, A.add)
+    ts(R("sg", 32, 64), R("vc", 32, 64), 64 * UP, A.mult, -8192 * UP, A.add)
+    quant("uq", "us", "ut")
     tt(R("w32"), R("sg", 32, 64), R("wmask"), A.mult)
+    act(col(CO), pw(WLO), F.Identity, scale=col(CG))
     act(col(C31), col(CL), F.Identity, bias=31.0, scale=-1.0)
     act(col(CEQ), col(CL), F.Identity, bias=-31.0, scale=2.0)
     act(col(CB), col(CL), F.Identity, bias=-32.0, scale=2.0)
@@ -303,32 +313,44 @@ def rank_program(g, core, T, topo):
     act(col(CW), pw(WF), F.Copy, scale=-UP / 2)
     act(R("ones"), R("qrow"), F.Identity, bias=1.0, scale=0.0)
     add("g", lambda: g.affine_select(T.ident[:], T.ones[:], [[-1, 128]], A.is_equal, 0.0, 0, 1), [R("ones")], [R("ident")])
-    for k in range(2):
-        act(R("a%d" % k, 0, 1), col(CL), F.Copy, scale=0.0)
-        act(R("a%d" % k, 385, 416), R("near", 0, 31), F.Relu, bias=1024.0, scale=-1024.0)
-        act(R("b%d" % k, 384, 416), R("near"), F.Relu, bias=1022.0, scale=-1022.0)
-    for lo in range(0, 128, 32):
-        hi = lo + 32
-        add("a", lambda lo=lo, hi=hi: S.activation(T.fm[lo:hi, 4 * lo:4 * hi:4], T.sg[lo:hi, 0:32], F.Identity, scale=T.col[lo:hi, CO:CO + 1]),
-            [R("sg", 0, 32), col(CO)], [R("fm", 4 * lo, 4 * hi, 4)])
-    for lo in range(0, 128, 32):
-        hi = lo + 32
-        add("a", lambda lo=lo, hi=hi: S.activation(T.fm[lo:hi, 512 + 4 * lo:512 + 4 * hi:4], T.w32[lo:hi, :], F.Copy),
-            [R("w32")], [R("fm", 512 + 4 * lo, 512 + 4 * hi, 4)])
-    quant("uq", "us", "ut")
+    blocks(0, "sg", CO)
+    blocks(512, "w32", None)
     quant("xq0", "xs0", "x0", *SPANS[0])
     for t in range(ROUNDS):
         x, xq, xs = "x%d" % t, "xq%d" % t, "xs%d" % t
         p, pq, pp, nq, npl = "p%d" % t, "pq%d" % t, "pp%d" % t, "nq%d" % t, "np%d" % t
         first = t == 0
         s0, s1 = SPANS
+        ends = R("lpos", 24, 26)
 
-        def layer(b):
-            mm(b, "wq", "wp", b, xq, xs)
+        def cast(b):
             act(R(p, b, 4 * C, 4), bank(b), F.Copy, scale=0.03125)
 
         def key(lo, hi):
             tt(R("key", lo, hi), R("ps", 512 * 7 + lo, 512 * 7 + hi), R("wcon", lo, hi), A.add)
+
+        def ask(lo, hi):
+            tt(R("dg", lo, hi), R("ps", 512 * 4 + lo, 512 * 4 + hi), R("diag", lo, hi), A.mult)
+
+        def part(lo):
+            quant(pq, pp, p, lo, lo + 128)
+            send(nq, pq, "gotp%d" % t, lo, lo + 128, codes=True)
+
+        def lowest(k, at):
+            tt(R("firsts", at, at + 32), (R("ymin", 392 * k, 392 * k + 385), ends), R("crow", 32 * min(k, 1), 32 * min(k, 1) + 32), A.subtract)
+
+        def spread(k, at):
+            for d in range(2):
+                turn(R("ta", 64 * k + d, 64 * k + 64, 2), R("firsts", at, at + 32))
+
+        def above(k, at):
+            turn(R("firsts", at - 32, at), R("ta", 64 * k, 64 * k + 64))
+
+        def below(k, at):
+            turn(R("firsts", at + 32, at + 64), R("ta", 64 * k, 64 * k + 63))
+
+        def found(b, lo, hi):
+            return (R("dwin", 392 * b, 392 * b + 385), R("lfound", lo // 16, hi // 16))
 
         mm(4, "uq", "us", 0, xq, xs, *s0)
         quant(xq, xs, x, *s1)
@@ -336,15 +358,18 @@ def rank_program(g, core, T, topo):
         for k, (lo, hi) in enumerate(SPANS):
             act(R("bits", 4 * lo, 4 * hi, 4), bank(4 + k, hi - lo), F.Sign, bias=TINY)
         if first:
+            for k in range(2):
+                act(R("a%d" % k, 0, 1), col(CL), F.Copy, scale=0.0)
+                act(R("a%d" % k, 385, 416), R("near", 0, 31), F.Relu, bias=1024.0, scale=-1024.0)
+                act(R("b%d" % k, 384, 416), R("near"), F.Relu, bias=1022.0, scale=-1022.0)
             quant("fq", "fs", "fm", 256, 512, 0)
-            tt(R("tint", 9, 10), R("tint", 8, 9), R("pint", 4, 5), A.add)
+            ts(R("fm", 0, 512, 4), R("grow"), col(CGI), A.is_equal, col(CW), A.mult)
         else:
-            layer(0)
+            mm(0, "wq", "wp", 0, xq, xs)
+            cast(0)
         quant("bq", "bs", "bits", *s0)
         mm(2, "fq", "fs", 0, "bq", "bs", *s0)
         mm(6, "fq", "fs", 2, "bq", "bs", *s0)
-        if first:
-            ts(R("fm", 0, 512, 4), R("grow"), col(CGI), A.is_equal, col(CW), A.mult)
         quant("bq", "bs", "bits", *s1)
         mm(3, "fq", "fs", 0, "bq", "bs", *s1)
         mm(1, "fq", "fs", 2, "bq", "bs", *s1)
@@ -352,19 +377,22 @@ def rank_program(g, core, T, topo):
         mm(5, "fq", "fs", 1, "bq", "bs")
         if first:
             quant("fq", "fs", "fm", 512, 640, 0)
+            mm(0, "wq", "wp", 0, xq, xs)
         mm(7, "fq", "fs", 3, "bq", "bs", tiles=2)
         ts(R("a0", 1, 1 + s0[1]), bank(2, s0[1]), col(CEQ), A.is_equal, 1024.0, A.mult)
         act(R("a1", 1, 1 + s0[1]), bank(6, s0[1]), F.Relu, bias=-512.0 * 29, scale=512.0)
+        act(R("a1", 1 + s1[0], 1 + C), bank(1, C - s1[0]), F.Relu, bias=-512.0 * 29, scale=512.0)
         act(R("junk", 0, C), bank(4), F.Sign, bias=col(CB), scale=-1.0, acc=R("base", 0, 1))
         act(R("junk", C, 2 * C), bank(5), F.Sign, bias=col(CB), scale=-1.0, acc=R("base", 1, 2))
         ts(R("a0", 1 + s1[0], 1 + C), bank(3, C - s1[0]), col(CEQ), A.is_equal, 1024.0, A.mult)
-        if first:
-            ts(R("tint", 10, 11), R("tint", 9, 10), 15, A.bitwise_and)
-        ts(R("a1", 1 + s1[0], 1 + C), bank(1, C - s1[0]), 31.0, A.is_equal, 1024.0, A.mult)
-        ts(R("b0", 0, C), R("a0", 1, 1 + C), 1022.0 / 1024, A.mult)
+        ts(R("b0", *s0), R("a0", 1, 1 + s0[1]), 1022.0 / 1024, A.mult)
+        ts(R("b0", *s1), R("a0", 1 + s1[0], 1 + C), 1022.0 / 1024, A.mult)
         ts(R("b1", 0, C), R("a1", 1, 1 + C), 1022.0 / 1024, A.mult)
-        for b in ((0, 3, 1, 2) if first else (3, 1, 2)):
-            layer(b)
+        if first:
+            cast(0)
+        for b in (3, 1, 2):
+            mm(b, "wq", "wp", b, xq, xs)
+            cast(b)
         if not first:
             mm(4, "eq", "es", 4, "bq", "bs")
         scan(R("cnt", 0, 416), R("a0"), R("b0"), 0.0, A.add, A.subtract)
@@ -374,131 +402,140 @@ def rank_program(g, core, T, topo):
         key(0, 192)
         if first:
             fill(R("ymin", 0, 3 * 392, 392), HUGE)
-            for k in range(3):
-                fill(R("ymin", 392 * k + 385, 392 * k + 392), HUGE)
             act(R("crow", 0, 32), R("vrow", 0, 32), F.Identity, bias=-UP * MID, scale=64 * UP)
             act(R("crow", 32, 64), R("vrow", 0, 32), F.Identity, bias=-UP * (MID + 8192), scale=64 * UP)
-            act(col(C64), col(CG), F.Copy, scale=64.0)
-            fill(R("firsts", 64, 96), 0.0)
-            fill(R("ta", 0, 64), 0.0)
-            fill(R("ta", 160, 224), 0.0)
-            fill(R("ta", 256, 320), 0.0)
             act(col(CNL), pw(WLO), F.Copy, scale=0.5)
-            act(R("em", 2048, 2560), R("fm", 0, 512), F.Copy, scale=0.0)
-            act(col(CF), pw(WF), F.Identity, bias=col(CNL), scale=-18.0)
-            for lo in (0, 1024):
-                act(R("em", lo, lo + 1024), R("fm"), F.Copy, scale=0.0)
-            act(R("r16"), R("k16"), F.Sign)
-            for b in range(4):
-                act(R("em", 512 * b + b, 512 * b + 512, 4), R("ident"), F.Copy)
-            fill(R("k512"), 512.0)
-            fill(R("dist", 34, 288, 36), 4096.0)
-            fill(R("dist", 35, 288, 36), 4096.0)
-            fill(R("dwin", 0, 4 * 392, 392), 0.0)
-            for b in range(4):
-                fill(R("dwin", 392 * b + 385, 392 * b + 392), 0.0)
         turn(R("zt", 0, 416), R("cum", 0, 416))
         turn(R("zt", 416, 832), R("cum", 416, 832))
         scan(R("zs", 0, 416), R("r32"), R("zt", 0, 416), 0.0, A.max, A.min)
         scan(R("zs", 416, 832), R("r32"), R("zt", 416, 832), 0.0, A.max, A.min)
         key(192, C)
-        act(R("him"), R("key"), F.Relu, bias=MISS - MID, scale=-1.0 / UP)
+        if first:
+            act(col(CD), col(CG), F.Identity, bias=1.0, scale=1.0 / 2048 - 1)
+            act(col(CU), col(CG), F.Identity, bias=1.0, scale=2047.0)
+            act(col(CN), col(CG), F.Identity, bias=1.0, scale=-1.0)
+            act(col(CF), pw(WF), F.Identity, bias=col(CNL), scale=-18.0)
+            act(col(CP), col(CD), F.Copy, scale=1536.0)
+        act(R("him", 0, C), R("key"), F.Relu, bias=MISS - MID, scale=-1.0 / UP)
+        act(R("him", C, ASK), R("key", 0, 16), F.Relu, bias=MISS - MID, scale=-1.0 / UP)
+        if first:
+            act(R("fm", 512, 1024, 4), R("ident"), F.Copy)
+            for lo in (0, 768):
+                act(R("em", lo, lo + 768), R("junk"), F.Copy, scale=0.0)
+            act(R("r16"), R("k16"), F.Sign)
+            for b in range(1, 4):
+                act(R("em", 512 * (b - 1) + b, 512 * b, 4), R("ident"), F.Copy)
+            act(R("dgs"), R("k16"), F.Abs, bias=col(CI), scale=-1.0)
+            act(R("m32"), R("r16"), F.Copy)
+            act(R("diag"), R("dgs"), F.Relu, bias=1.0, scale=-1.0)
+            act(col(CK), col(CD), F.Copy, scale=512.0)
+            act(R("hb"), R("hrow"), F.Identity, scale=col(CD))
+            fill(R("m32", 16, C, 32), col(CN))
+            fill(R("k512"), col(CK))
+            fill(R("dist", 34, 288, 36), 4096.0)
+            fill(R("dist", 35, 288, 36), 4096.0)
+            fill(R("dwin", 0, 4 * 392, 392), 0.0)
         ts(R("lpos", 0, 26), R("zs", 31, 832, 32), 1406.0, A.add, 0.5, A.mult)
-        ends = R("lpos", 24, 26)
-        quant(pq, pp, p, 0, 128)
-        send(nq, pq, "gotp%d" % t, 0, 128, codes=True)
+        part(0)
         copy((R("srt"), R("lpos", 0, 24)), R("key"))
-        quant(pq, pp, p, 128, 256)
+        part(128)
         scan(R("ymin", 1, 385), R("srt"), R("srt"), HUGE, A.min, A.min)
-        quant(pq, pp, p, 256, C)
-        send(nq, pq, "gotp%d" % t, 128, C, codes=True)
-        send(npl, pp, "gotp%d" % t)
+        part(256)
+        lowest(0, 32)
         scan(R("ymin", 393, 777), R("srt"), R("ymin", 0, 384), HUGE, A.min, A.max)
-        if first:
-            copy(col(CSH), R("tint", 10, 11))
-        tt(R("firsts", 32, 64), (R("ymin", 0, 392), ends), R("crow", 0, 32), A.subtract)
-        tt(R("firsts", 96, 128), (R("ymin", 392, 784), ends), R("crow", 32, 64), A.subtract)
-        if first:
-            ts(R("lsh"), R("row16"), col(CSH), A.add, col(C64), A.add)
+        spread(0, 32)
+        lowest(1, 128)
         scan(R("ymin", 785, 1169), R("srt"), R("ymin", 392, 776), HUGE, A.min, A.max)
-        turn(R("ta", 64, 160), R("firsts", 32, 128))
-        tt(R("firsts", 160, 192), (R("ymin", 784, 1176), ends), R("crow", 32, 64), A.subtract)
-        copy(R("tb", 0, 96), (R("ta", 0, 224), R("lsh", 0, 6)))
-        turn(R("ta", 224, 256), R("firsts", 160, 192))
-        if first:
-            ts(R("em", 2048, 2560, 4), R("grow"), col(CGI), A.is_equal, col(CF), A.mult)
-        for k in (1, 2, 0):
-            turn(R("firsts", 64 * k, 64 * k + 32), R("tb", 32 * k, 32 * k + 32))
-        copy(R("tb", 96, 128), (R("ta", 224, 320), R("lsh", 0, 2)))
-        ts(R("r2"), R("firsts", 95, 129), -4096.0 * UP, A.add)
-        tt(R("r1"), R("firsts", 96, 130), R("firsts", 31, 65), A.max)
-        turn(R("firsts", 192, 224), R("tb", 96, 128))
+        spread(1, 128)
+        above(0, 32)
+        lowest(2, 192)
+        above(1, 128)
+        below(1, 128)
+        below(0, 32)
+        spread(2, 192)
+        ts(R("r2"), R("firsts", 127, 161), -4096.0 * UP, A.add)
+        tt(R("r1"), R("firsts", 128, 162), R("firsts", 31, 65), A.max)
+        below(2, 192)
         tt(R("r4"), R("r2"), R("firsts", 30, 64), A.min)
-        tt(R("r3"), R("r1"), R("firsts", 160, 194), A.min)
         if first:
-            quant("eq", "es", "em", 512, 640)
+            ts(R("fm", 0, 512, 4), R("grow"), col(CGI), A.is_equal, col(CF), A.mult)
+        tt(R("r3"), R("r1"), R("firsts", 192, 226), A.min)
+        if first:
+            quant("eq", "es", "fm", 512, 640, 0)
             mm(4, "eq", "es", 4, "bq", "bs")
+        else:
+            ask(0, 128)
         tt(R("vi"), R("r3"), R("r4"), A.min)
         if first:
-            ts(R("diag"), R("k16"), col(CI), A.is_equal)
+            quant("eq", "es", "fm", 0, 128, 128)
+        else:
+            ask(128, 256)
         ts(R("vf"), R("vi"), 0x7E003800, A.bitwise_and)
         ts(R("vn"), R("vi"), 14, A.logical_shift_right, 511, A.bitwise_and)
         if first:
-            quant("eq", "es", "em", 0, 128)
+            ts(R("tint", 5, 6), p0, 15, A.bitwise_and, 1, A.logical_shift_right)
+            ts(R("tint", 6, 7), R("pint", 2, 3), 16, A.bitwise_and)
+        else:
+            ask(256, C)
         tt(R("tab%d" % t), R("vf"), R("vn"), A.add)
         send("land%d" % t, "tab%d" % t, "gott%d" % t)
+        send(npl, pp, "gotp%d" % t)
         if first:
-            copy(col(CH), R("tint", 5, 6))
-            ts(R("tint", 6, 8), R("pint", 2, 4), 16, A.bitwise_and)
-            act(col(CB2), col(CH), F.Identity, bias=col(CG), scale=2.0)
-            act(col(CB3), col(CB2), F.Identity, bias=16.0)
-        tt(R("dg"), bank(4), R("diag"), A.mult)
+            ask(0, C)
+            copy(R("col", CH, CH + 2), R("tint", 5, 7))
+            memset(R("fj", 24, 32), 0)
+        scan(R("dgs"), R("r16"), R("dg"), 0.0, A.mult, A.add)
         if first:
-            quant("eq", "es", "em", 128, 512)
+            act(col(CB2), col(CG), F.Identity, bias=0.75, scale=-1.0 / 16)
+            act(col(CB3), col(CL), F.Abs, bias=-16.0)
+            act(col(CT), col(CX), F.Identity, bias=col(CH), scale=col(CB2))
+            act(col(CZ), col(CB3), F.Relu, bias=12.0, scale=-12.0)
+            quant("eq", "es", "em", 128, 256, 0)
         else:
             quant("vq", "vs", "vt")
-        scan(R("dgs"), R("r16"), R("dg"), 0.0, A.mult, A.add)
-        ts(R("lask"), R("dgs", 15, C, 16), 143.5, A.add)
+        ts(R("cap"), R("him"), col(CP), A.min)
+        ts(R("lask", 0, 24), R("dgs", 15, C, 16), 143.5, A.add)
+        ts(R("lask", 24, 25), R("dgs", 15, 16), 143.5, A.add)
+        for h in range(1, 8):
+            act(R("dist", 36 * h, 36 * h + 34), R("land%d" % t), F.Abs, bias=R("hb", h, h + 1), scale=col(CD))
+            if h == 4:
+                ts(R("dist", 0, 34), R("land%d" % t), 1.0, A.add, col(CD), A.mult)
+                if first:
+                    quant("eq", "es", "em", 256, 384, 128)
+                scan(R("ans", 0, 180), R("k512", 0, 180), R("dist", 0, 180), 4096.0, A.add, A.min)
+        scan(R("ans", 180, 288), R("k512", 180, 288), R("dist", 180, 288), 4096.0, A.add, A.min)
+        if first:
+            quant("eq", "es", "em", 384, 512, 256)
         for b in range(4):
             mm(b, "eq", "es", b, nq, npl)
-        for h in range(1, 8):
-            act(R("dist", 36 * h, 36 * h + 34), R("land%d" % t), F.Abs, bias=1.0 - 2048 * h)
-            if h == 3:
-                ts(R("dist", 0, 34), R("land%d" % t), 1.0, A.add)
-                if first:
-                    ts(R("lq", 0, 1), R("tint", 6, 7), 4.0, A.mult, col(CB2), A.add)
-                    ts(R("lq", 1, 2), R("tint", 7, 8), 4.0, A.mult, col(CB3), A.add)
-                scan(R("ans", 0, 144), R("k512"), R("dist", 0, 144), 4096.0, A.add, A.min)
-        if first:
-            memset(R("fj", 24, 32), 0)
-        scan(R("ans", 144, 288), R("k512"), R("dist", 144, 288), 4096.0, A.add, A.min)
-        if first:
-            memset(R("fj", 56, 64), 0)
-        tt(R("z2", *s0), (R("ans"), R("lask", 0, s0[1] // 16)), R("him", *s0), A.min)
-        act(R("zg", *s1), (R("ans"), R("lask", s1[0] // 16, C // 16)), F.Copy)
+        cut = s1[0]
+        tt(R("z2", 0, cut), (R("ans"), R("lask", 0, cut // 16)), R("cap", 0, cut), A.min)
+        act(R("zg", cut, ASK), (R("ans"), R("lask", cut // 16, ASK // 16)), F.Copy)
         for b in range(4):
             act(R("dwin", 392 * b + 1, 392 * b + 385), bank(b), F.Copy)
-        tt(R("z2", *s1), R("zg", *s1), R("him", *s1), A.min)
-        for lo, hi in SPANS:
-            turn(R("zt2", lo, hi), R("z2", lo, hi))
-        for lo, hi in SPANS:
-            scan(R("zs2", lo, hi), R("r16", lo, hi), R("zt2", lo, hi), 0.0, A.mult, A.max)
-        ts(R("fi"), R("zs2", 15, C, 16), 1536.0, A.min)
+        tt(R("z2", cut, ASK), R("zg", cut, ASK), R("cap", cut, ASK), A.min)
+        pieces = ((0, 0, cut), (C, 16, cut - 32), (cut, cut, C - cut), (C + cut - 32, cut - 16, C + 32 - cut))
+        for at, lo, w in pieces:
+            turn(R("zt2", at, at + w), R("z2", lo, lo + w))
+        for at, lo, w in pieces:
+            scan(R("zs2", at, at + w), R("m32", 0, w), R("zt2", at, at + w), 0.0, A.mult, A.max)
+        if first:
+            ts(R("lq", 0, 1), col(CT), col(CZ), A.add)
+            ts(R("lq", 1, 2), col(CT), 8.0, A.add)
+        ts(R("fi"), R("zs2", 31, 2 * C, 32), col(CU), A.mult)
         ts(R("fj", 0, 24), R("fi"), 511, A.bitwise_and)
-        ts(R("fj", 32, 56), R("fi"), 511, A.bitwise_and)
-        turn(R("fu"), R("fj", 0, 64))
-        turn(R("fj", 64, 96), R("fu", 16, 48))
         copy(R("lfound"), (R("fj"), R("lq")))
         nx = "x%d" % (t + 1)
-        for k, (lo, hi) in enumerate(SPANS):
-            found = R("lfound", lo // 16, hi // 16)
-            for b in range(2 - 2 * k, 4):
-                act(R("mg", C * b + lo, C * b + hi), (R("dwin", 392 * b, 392 * b + 392), found), F.Copy)
-            for b in range(4):
-                src = (R("dwin", 392 * b, 392 * b + 392), found) if b < 2 - 2 * k else R("mg", C * b + lo, C * b + hi)
+        mid = cut + 64
+        for lo, hi, bs in ((0, cut, (2, 3)), (mid, C, (0,)), (cut, C, (1, 2, 3))):
+            for b in bs:
+                act(R("mg", C * b + lo, C * b + hi), found(b, lo, hi), F.Copy)
+        for lo, hi, bs, own in ((0, cut, (0, 1), 1), (0, cut, (2, 3), 0), (cut, mid, (0,), 1), (mid, C, (0,), 0), (cut, C, (1, 2, 3), 0)):
+            if lo == mid:
+                quant("xq%d" % (t + 1), "xs%d" % (t + 1), nx, *s0)
+            for b in bs:
+                src = found(b, lo, hi) if own else R("mg", C * b + lo, C * b + hi)
                 tt(R(nx, 4 * lo + b, 4 * hi, 4), src, R(p, 4 * lo + b, 4 * hi, 4), A.add)
-                if k == 1 and b == 0:
-                    quant("xq%d" % (t + 1), "xs%d" % (t + 1), nx, *SPANS[0])
 
     x, xq, xs = "x%d" % ROUNDS, "xq%d" % ROUNDS, "xs%d" % ROUNDS
     outs = [("out", k, k + 1, 1) for k in range(8)]
@@ -512,5 +549,5 @@ def rank_program(g, core, T, topo):
                 dma("sa"[m % 2], lambda m=m: T.osc[4 * m:4 * m + 4, :], lambda m=m: T[xs][32 * m:32 * m + 4, :], [R(xs)], [outs[4 + m]])
         act(R("yb", lo, hi), bank(5 + k, hi - lo), F.Copy)
         dma("a", lambda lo=lo, hi=hi: T.y[:, lo:hi], lambda lo=lo, hi=hi: T.yb[:, lo:hi], [R("yb", lo, hi)], [outs[2 + k]])
-    add("g", lambda: g.wait_ge(T.sem.sent, 4 * ROUNDS * lanes_out), outs, [], "end")
+    add("g", lambda: g.wait_ge(T.sem.sent, 5 * ROUNDS * lanes_out), outs, [], "end")
     emit(g, T, ops)

from concourse.mybir import dt, AluOpType as A, ActivationFunctionType as F

C = 384
ROUNDS = 2
H16 = "float16"
X4 = "float8_e4m3fn_x4"
SPANS = ((0, 256), (256, C))
UP = 2048.0
MISS = 524288.0
MID = 8192.0 * 31 + 2 * MISS + 3.5
HUGE = UP * (MISS - MID)
TINY = 1e-37
ASK = C + 16


def sb(n, dtype):
    return ("sbuf", [128, n], dtype)


SCRATCH = {
    "ps": ("psum", [128, 4096], "float32"),
    "ut": sb(512, "bfloat16"), "vt": sb(512, "bfloat16"), "uq": sb(128, X4), "us": sb(128, "uint8"),
    "vq": sb(128, X4), "vs": sb(128, "uint8"), "wq": sb(512, X4), "wp": sb(512, "uint8"),
    "fm": sb(1024, "bfloat16"), "fq": sb(640, X4), "fs": sb(640, "uint8"),
    "em": sb(1536, "bfloat16"), "eq": sb(640, X4), "es": sb(640, "uint8"),
    "pint": sb(8, "int32"), "tint": sb(12, "int32"), "col": sb(32, "float32"),
    "krow": sb(48, "float32"), "eqm": sb(48, "float32"), "mul": sb(48, "float32"), "pw": sb(48, "float32"),
    "vrow": sb(64, "float32"), "vb": sb(64, "int32"), "vc": sb(64, "int32"), "sg": sb(64, "bfloat16"), "near": sb(32, "float32"),
    "qrow": sb(128, "bfloat16"), "grow": sb(128, "bfloat16"), "wmask": sb(32, "bfloat16"), "w32": sb(32, "bfloat16"),
    "qe": sb(128, "bfloat16"), "qo": sb(128, "bfloat16"), "ones": sb(128, "bfloat16"), "ident": sb(128, "bfloat16"),
    "wcon": sb(C, "float32"), "k16": sb(C, "bfloat16"), "diag": sb(C, "bfloat16"),
    "r32": sb(416, "bfloat16"), "r16": sb(C, "bfloat16"), "m32": sb(C, "bfloat16"), "k512": sb(288, "bfloat16"),
    "crow": sb(64, "float32"), "hrow": sb(8, "float32"), "hb": sb(8, "float32"), "lq": sb(2, "uint16"),
    "bits": sb(4 * C, "bfloat16"), "bq": sb(C, X4), "bs": sb(C, "uint8"),
    "a0": sb(416, "bfloat16"), "a1": sb(416, "bfloat16"), "b0": sb(416, H16), "b1": sb(416, H16),
    "cnt": sb(832, H16), "cum": ("sbuf", [128, 26, 32], H16), "base": sb(2, "float32"), "junk": sb(2 * C, "bfloat16"),
    "key": sb(C, "float32"), "srt": sb(C, "float32"), "zt": sb(832, H16), "zs": sb(832, H16), "lpos": sb(32, "uint16"),
    "ymin": sb(3 * 392, "float32"), "firsts": sb(256, "float32"), "ta": ("sbuf", [128, 6, 32], "float32"),
    "r1": sb(34, "float32"), "r2": sb(34, "float32"), "r3": sb(34, "float32"), "r4": sb(34, "float32"),
    "vi": sb(34, "int32"), "vf": sb(34, "int32"), "vn": sb(34, "int32"),
    "him": sb(ASK, "bfloat16"), "cap": sb(ASK, H16), "dg": sb(C, H16), "dgs": sb(C, H16), "lask": sb(26, "uint16"),
    "dist": sb(288, "float32"), "ans": sb(288, "float32"), "zg": sb(ASK, H16),
    "z2": sb(ASK, H16), "zt2": sb(2 * C, H16), "zs2": sb(2 * C, H16), "fi": sb(24, "int32"), "fj": sb(32, "int32"),
    "lfound": sb(32, "uint16"), "dwin": sb(4 * 392, "float32"), "mg": sb(4 * C, "bfloat16"), "yb": sb(C, "float32"),
}
for _t in range(ROUNDS + 1):
    SCRATCH["x%d" % _t] = sb(4 * C, "bfloat16")
    SCRATCH["xq%d" % _t] = sb(C, X4)
    SCRATCH["xs%d" % _t] = sb(C, "uint8")
for _t in range(ROUNDS):
    SCRATCH["p%d" % _t] = sb(4 * C, "bfloat16")
    SCRATCH["pq%d" % _t] = sb(C, X4)
    SCRATCH["pp%d" % _t] = sb(C, "uint8")
    SCRATCH["nq%d" % _t] = sb(C, X4)
    SCRATCH["np%d" % _t] = sb(C, "uint8")
    SCRATCH["tab%d" % _t] = sb(34, "float32")
    SCRATCH["land%d" % _t] = sb(34, "float32")

NPOOL = 120
SEMAPHORES = ["s%d" % _i for _i in range(NPOOL)] + ["sent"] + ["gotp%d" % _t for _t in range(ROUNDS)] + ["gott%d" % _t for _t in range(ROUNDS)]

CI, CL, CG, CGI, CQ, CB2, CB3, C31, CB, CEQ, CW, CNL, CF, CO, CH, CX, CD, CU, CK, CT, CP, CN, CZ = range(23)
WLO, WF, W9, PSH = 15, 6, 31, 47


def meet(r, s):
    if r[0] != s[0]:
        return False
    if r[0] == "ps":
        return r[1] // 512 <= (s[2] - 1) // 512 and s[1] // 512 <= (r[2] - 1) // 512
    if r[2] <= s[1] or s[2] <= r[1]:
        return False
    return not (r[3] == s[3] and r[3] > 1 and (r[1] - s[1]) % r[3])


def emit(g, T, ops):
    queues = {"g": g, "v": g.vector, "a": g.scalar, "t": g.tensor, "s": g.sync}
    known = {k: set() for k in queues}
    before, waits, needed = [], [], set()
    for i, (q, kind, fn, rd, wr) in enumerate(ops):
        deps = []
        for j in range(i - 1, -1, -1):
            if j in known[q]:
                continue
            q2, kind2, _, rd2, wr2 = ops[j]
            hit = any(meet(r, s) for r in rd + wr for s in wr2) or any(meet(r, s) for r in wr for s in rd2)
            if not hit and q2 != q:
                hit = any(r[0] == "ps" and meet(r, s) for r in rd for s in rd2)
            if hit:
                deps.append(j)
                known[q] = known[q] | before[j] | {j}
        waits.append(deps)
        needed.update(deps)
        before.append(set() if kind == "arrive" else known[q])
    team, seen = {}, set()
    for i in range(len(ops)):
        fresh = [j for j in waits[i] if j not in seen and ops[j][1] == "op"]
        seen.update(waits[i])
        for j in fresh:
            team[j] = fresh
    last, mark = [], {}
    for i, (q, kind, fn, rd, wr) in enumerate(ops):
        if kind == "arrive":
            mark[i] = fn
            continue
        for m in sorted(set(mark[j] for j in waits[i])):
            queues[q].wait_ge(T.sem[m[0]], m[1])
        call = fn()
        if i in needed:
            mates = team.get(i, [i])
            if i not in mark:
                k = len(last)
                if kind == "op":
                    for n in range(len(last)):
                        if last[n][2] == "op" and all(j in before[m] for j in last[n][0] for m in mates):
                            k = n
                            break
                if k == len(last):
                    last.append(([], 0, kind))
                last[k] = (mates, last[k][1] + (len(mates) if kind == "op" else 16), kind)
                for m in mates:
                    mark[m] = ("s%d" % k, last[k][1])
            call.then_inc(T.sem[mark[i][0]], 1 if kind == "op" else 16)


def rank_program(g, core, T, topo):
    rank = T.rank_of(core)
    if rank is None:
        return
    n = len(T.cores)
    to = T.cores[(rank - 1) % n]
    frm = T.cores[(rank + 1) % n]
    rid, pid, _ = topo.addr(to)
    mask = topo.mask(core, to)
    lanes_out, lanes_in = len(topo.engines(core, to)), len(topo.engines(frm, core))
    ops = []
    V, S, PE = g.vector, g.scalar, g.tensor

    def R(name, lo=0, hi=None, step=1):
        return (name, lo, SCRATCH[name][1][1] if hi is None else hi, step)

    def col(k):
        return R("col", k, k + 1)

    def pw(k):
        return R("pw", k, k + 1)

    def bank(k, w=C):
        return R("ps", 512 * k, 512 * k + w)

    def ap(r):
        if not isinstance(r, tuple):
            return r
        if len(r) == 2:
            return ap(r[0]).indirect(ap(r[1]))
        if r[0] == "cum":
            return T.cum[:, :, 16 * r[1]:16 * r[1] + 16] if r[3] == 2 else T.cum[:, r[1] // 32:r[2] // 32, :]
        if r[0] == "ta":
            k = r[1] // 64
            c = 16 * (r[1] % 64) if r[3] == 2 else (15 if r[2] % 64 else 1)
            return T.ta[:, 2 * k:2 * k + 2, c:c + 16]
        return T[r[0]][:, r[1]:r[2]:r[3]] if r[3] > 1 else T[r[0]][:, r[1]:r[2]]

    def runs(*rs):
        out = []
        for r in rs:
            if isinstance(r, tuple):
                out += list(r) if len(r) == 2 else [r]
        return out

    def add(q, fn, rd, wr, kind="op"):
        ops.append((q, kind, fn, rd, wr))

    def memset(o, c):
        add("v", lambda: V.memset(ap(o), c), [], [o])

    def copy(o, i):
        if len(o) == 2:
            add("v", lambda: V.tensor_copy(ap(o), ap(i)), runs(i, o[1]), [o[0]])
        else:
            add("v", lambda: V.tensor_copy(ap(o), ap(i)), runs(i), [o])

    def ts(o, i, s1, op0, s2=None, op1=None):
        if op1 is None:
            add("v", lambda: V.tensor_scalar(ap(o), ap(i), ap(s1), None, op0), runs(i, s1), [o])
        else:
            add("v", lambda: V.tensor_scalar(ap(o), ap(i), ap(s1), ap(s2), op0, op1), runs(i, s1, s2), [o])

    def tt(o, i0, i1, op):
        add("v", lambda: V.tensor_tensor(ap(o), ap(i0), ap(i1), op), runs(i0, i1), [o])

    def scan(o, d0, d1, init, op0, op1):
        add("v", lambda: V.tensor_tensor_scan(ap(o), ap(d0), ap(d1), ap(init), op0, op1), runs(d0, d1, init), [o])

    def turn(o, i):
        add("v", lambda: V.transpose(ap(o), ap(i)), [i], [o])

    def quant(c, s, i, lo=0, hi=None, at=None):
        hi = SCRATCH[c][1][1] if hi is None else hi
        at = lo if at is None else at
        a, b, d = R(c, lo, hi), R(s, lo, hi), R(i, 4 * at, 4 * (at + hi - lo))
        add("v", lambda: V.quantize_mx(ap(a), ap(b), ap(d)), [d], [a, b])

    def act(o, i, func, bias=None, scale=None, acc=None):
        kw = {}
        if bias is not None:
            kw["bias"] = bias
        if scale is not None:
            kw["scale"] = scale
        if acc is not None:
            kw["accum_out"] = acc
        add("a", lambda: S.activation(ap(o), ap(i), func, **{k: ap(w) for k, w in kw.items()}), runs(i, bias, scale), runs(o, acc))

    def fill(o, c, src="r32"):
        act(o, R(src, 0, len(range(o[1], o[2], o[3]))), F.Identity, bias=c, scale=0.0)

    def mm(k, lq, ls, at, rq, rs, lo=0, hi=C, tiles=1):
        o = bank(k, hi - lo)
        rd = [R(lq, 128 * at, 128 * (at + tiles)), R(ls, 128 * at, 128 * (at + tiles)), R(rq, lo, hi), R(rs, lo, hi)]

        def call():
            for m in range(at, at + tiles):
                last = PE.matmul_mx(ap(o), ap(R(lq, 128 * m, 128 * m + 128)), ap(R(ls, 128 * m, 128 * m + 128)), ap(rd[2]), ap(rd[3]),
                                    m == at, m == at + tiles - 1)
            return last
        add("t", call, rd, [o])

    def iota(o, pattern, base, mult):
        if SCRATCH[o[0]][2] == "int32":
            add("g", lambda: g.iota(ap(o), pattern, base, mult), [], [o])
        else:
            add("g", lambda: g.iota(ap(o), pattern, base, mult, allow_small_or_imprecise_dtypes=True), [], [o])

    def dma(q, out, in_, rd, wr):
        eng = {"a": S, "s": g.sync}[q]
        add(q, lambda: eng.dma_start(out(), in_()), rd, wr, "dma")

    def send(dst, src, sem, lo=0, hi=None, codes=False):
        def call():
            o, i = ap(R(dst, lo, hi)), ap(R(src, lo, hi))
            if codes:
                o, i = o.bitcast(dt.uint8), i.bitcast(dt.uint8)
            return g.remote_dma(o, i, T.sem[sem], T.sem.sent, pid, rid, mask)
        add("g", call, [R(src, lo, hi)], [], "send")

    def arrive(sem, count, bufs):
        add("g", (sem, count), [], [R(b) for b in bufs], "arrive")

    def blocks(at, src, scale):
        for lo in range(0, 128, 32):
            hi = lo + 32
            kw = {"scale": T.col[lo:hi, scale:scale + 1]} if scale is not None else {}
            add("a", lambda lo=lo, hi=hi, kw=kw: S.activation(T.fm[lo:hi, at + 4 * lo:at + 4 * hi:4], T[src][lo:hi, 0:32], F.Identity, **kw),
                [R(src, 0, 32)] + ([col(scale)] if scale is not None else []), [R("fm", at + 4 * lo, at + 4 * hi, 4)])

    for lo, hi in SPANS:
        dma("s", lambda lo=lo, hi=hi: T.x0[:, 4 * lo:4 * hi], lambda lo=lo, hi=hi: T.x[:, 4 * lo:4 * hi], [], [R("x0", 4 * lo, 4 * hi)])
    dma("a", lambda: T.ut[:], lambda: T.u[:], [], [R("ut")])
    dma("s", lambda: T.wp[:], lambda: T.ws[:], [], [R("wp")])
    for lo in (0, 256):
        dma("s", lambda lo=lo: T.wq[:, lo:lo + 256].bitcast(dt.uint8), lambda lo=lo: T.wc[:, 4 * lo:4 * lo + 1024], [], [R("wq", lo, lo + 256)])
    dma("s", lambda: T.vt[:], lambda: T.v[:], [], [R("vt")])
    for t in range(ROUNDS):
        arrive("gotp%d" % t, 4 * lanes_in, ["nq%d" % t, "np%d" % t])
        arrive("gott%d" % t, lanes_in, ["land%d" % t])

    iota(R("pint", 0, 1), [[0, 1]], 0, 1)
    iota(R("krow"), [[0, 3], [-1, 16]], 15, 0)
    iota(R("qrow"), [[1, 4], [0, 32]], 0, 0)
    iota(R("vrow", 0, 32), [[-256, 32]], 31 * 256, 0)
    iota(R("vrow", 32, 64), [[0, 2], [8192, 16]], 0, 0)
    iota(R("grow"), [[1, 8], [0, 16]], 0, 0)
    iota(R("wcon"), [[8 * int(UP), C]], 0, 0)
    iota(R("r32"), [[0, 13], [-2048, 32]], 0, 0)
    iota(R("pint", 2, 3), [[0, 1]], 0, 17)
    iota(R("hrow"), [[-2048, 8]], 1, 0)
    iota(R("k16"), [[0, 24], [1, 16]], 0, 0)
    p0 = R("pint", 0, 1)
    memset(R("junk", 0, C), 0.0)
    memset(R("fm", 0, 256), 0.0)
    for lo, hi, step, c in ((0, 16, 1, 2.0), (16, 27, 1, 1.0), (27, 32, 1, 2.0), (33, 48, 1, 0.5), (4, 12, 7, 0.0), (23, 33, 9, 0.0)):
        fill(R("mul", lo, hi, step), c, "junk")
    for b in range(1, 4):
        act(R("bits", b, 4 * C, 4), R("junk", 0, C), F.Copy)
    ts(R("tint", CI, CI + 1), p0, 15, A.bitwise_and)
    ts(R("tint", CG, CG + 1), p0, 4, A.logical_shift_right, 1, A.bitwise_and)
    ts(R("tint", CQ, CQ + 1), p0, 5, A.logical_shift_right)
    ts(R("tint", CL, CL + 1), p0, 31, A.bitwise_and)
    ts(R("tint", CGI, CGI + 1), p0, 4, A.logical_shift_right)
    memset(R("fm", 256, 640), 0.0)
    copy(R("col", 0, 5), R("tint", 0, 5))
    memset(R("fm", 640, 1024), 0.0)
    ts(R("eqm"), R("krow"), col(CI), A.is_equal)
    ts(R("qo"), R("qrow"), col(CQ), A.is_equal, col(CG), A.mult)
    ts(R("qe"), R("qrow"), col(CQ), A.is_equal)
    scan(R("pw"), R("mul"), R("eqm"), 0.0, A.mult, A.add)
    tt(R("qe"), R("qe"), R("qo"), A.subtract)
    ts(R("vb"), R("vrow"), pw(PSH), A.mult)
    ts(R("fm", 512, 1024, 4), R("qo"), pw(WLO), A.mult)
    ts(R("fm", 0, 512, 4), R("qe"), pw(WLO), A.mult)
    ts(R("vc"), R("vb"), 256, A.bitwise_and)
    ts(R("wmask"), R("grow", 0, 32), col(CG), A.is_equal, pw(W9), A.mult)
    quant("fq", "fs", "fm", 0, 256)
    ts(R("sg", 0, 32), R("vc", 0, 32), -1.0 / 128, A.mult, 1.0, A.add)
    ts(R("sg", 32, 64), R("vc", 32, 64), 64 * UP, A.mult, -8192 * UP, A.add)
    quant("uq", "us", "ut")
    tt(R("w32"), R("sg", 32, 64), R("wmask"), A.mult)
    act(col(CO), pw(WLO), F.Identity, scale=col(CG))
    act(col(C31), col(CL), F.Identity, bias=31.0, scale=-1.0)
    act(col(CEQ), col(CL), F.Identity, bias=-31.0, scale=2.0)
    act(col(CB), col(CL), F.Identity, bias=-32.0, scale=2.0)
    act(R("near"), R("vrow", 0, 32), F.Abs, bias=col(C31), scale=-1.0 / 256)
    act(col(CW), pw(WF), F.Copy, scale=-UP / 2)
    act(R("ones"), R("qrow"), F.Identity, bias=1.0, scale=0.0)
    add("g", lambda: g.affine_select(T.ident[:], T.ones[:], [[-1, 128]], A.is_equal, 0.0, 0, 1), [R("ones")], [R("ident")])
    blocks(0, "sg", CO)
    blocks(512, "w32", None)
    quant("xq0", "xs0", "x0", *SPANS[0])
    for t in range(ROUNDS):
        x, xq, xs = "x%d" % t, "xq%d" % t, "xs%d" % t
        p, pq, pp, nq, npl = "p%d" % t, "pq%d" % t, "pp%d" % t, "nq%d" % t, "np%d" % t
        first = t == 0
        s0, s1 = SPANS
        ends = R("lpos", 24, 26)

        def cast(b):
            act(R(p, b, 4 * C, 4), bank(b), F.Copy, scale=0.03125)

        def key(lo, hi):
            tt(R("key", lo, hi), R("ps", 512 * 7 + lo, 512 * 7 + hi), R("wcon", lo, hi), A.add)

        def ask(lo, hi):
            tt(R("dg", lo, hi), R("ps", 512 * 4 + lo, 512 * 4 + hi), R("diag", lo, hi), A.mult)

        def part(lo):
            quant(pq, pp, p, lo, lo + 128)
            send(nq, pq, "gotp%d" % t, lo, lo + 128, codes=True)

        def lowest(k, at):
            tt(R("firsts", at, at + 32), (R("ymin", 392 * k, 392 * k + 385), ends), R("crow", 32 * min(k, 1), 32 * min(k, 1) + 32), A.subtract)

        def spread(k, at):
            for d in range(2):
                turn(R("ta", 64 * k + d, 64 * k + 64, 2), R("firsts", at, at + 32))

        def above(k, at):
            turn(R("firsts", at - 32, at), R("ta", 64 * k, 64 * k + 64))

        def below(k, at):
            turn(R("firsts", at + 32, at + 64), R("ta", 64 * k, 64 * k + 63))

        def found(b, lo, hi):
            return (R("dwin", 392 * b, 392 * b + 385), R("lfound", lo // 16, hi // 16))

        mm(4, "uq", "us", 0, xq, xs, *s0)
        quant(xq, xs, x, *s1)
        mm(5, "uq", "us", 0, xq, xs, *s1)
        for k, (lo, hi) in enumerate(SPANS):
            act(R("bits", 4 * lo, 4 * hi, 4), bank(4 + k, hi - lo), F.Sign, bias=TINY)
        if first:
            for k in range(2):
                act(R("a%d" % k, 0, 1), col(CL), F.Copy, scale=0.0)
                act(R("a%d" % k, 385, 416), R("near", 0, 31), F.Relu, bias=1024.0, scale=-1024.0)
                act(R("b%d" % k, 384, 416), R("near"), F.Relu, bias=1022.0, scale=-1022.0)
            quant("fq", "fs", "fm", 256, 512, 0)
            ts(R("fm", 0, 512, 4), R("grow"), col(CGI), A.is_equal, col(CW), A.mult)
        else:
            mm(0, "wq", "wp", 0, xq, xs)
            cast(0)
        quant("bq", "bs", "bits", *s0)
        mm(2, "fq", "fs", 0, "bq", "bs", *s0)
        mm(6, "fq", "fs", 2, "bq", "bs", *s0)
        quant("bq", "bs", "bits", *s1)
        mm(3, "fq", "fs", 0, "bq", "bs", *s1)
        mm(1, "fq", "fs", 2, "bq", "bs", *s1)
        mm(4, "fq", "fs", 0, "bq", "bs")
        mm(5, "fq", "fs", 1, "bq", "bs")
        if first:
            quant("fq", "fs", "fm", 512, 640, 0)
            mm(0, "wq", "wp", 0, xq, xs)
        mm(7, "fq", "fs", 3, "bq", "bs", tiles=2)
        ts(R("a0", 1, 1 + s0[1]), bank(2, s0[1]), col(CEQ), A.is_equal, 1024.0, A.mult)
        act(R("a1", 1, 1 + s0[1]), bank(6, s0[1]), F.Relu, bias=-512.0 * 29, scale=512.0)
        act(R("a1", 1 + s1[0], 1 + C), bank(1, C - s1[0]), F.Relu, bias=-512.0 * 29, scale=512.0)
        act(R("junk", 0, C), bank(4), F.Sign, bias=col(CB), scale=-1.0, acc=R("base", 0, 1))
        act(R("junk", C, 2 * C), bank(5), F.Sign, bias=col(CB), scale=-1.0, acc=R("base", 1, 2))
        ts(R("a0", 1 + s1[0], 1 + C), bank(3, C - s1[0]), col(CEQ), A.is_equal, 1024.0, A.mult)
        ts(R("b0", *s0), R("a0", 1, 1 + s0[1]), 1022.0 / 1024, A.mult)
        ts(R("b0", *s1), R("a0", 1 + s1[0], 1 + C), 1022.0 / 1024, A.mult)
        ts(R("b1", 0, C), R("a1", 1, 1 + C), 1022.0 / 1024, A.mult)
        if first:
            cast(0)
        for b in (3, 1, 2):
            mm(b, "wq", "wp", b, xq, xs)
            cast(b)
        if not first:
            mm(4, "eq", "es", 4, "bq", "bs")
        scan(R("cnt", 0, 416), R("a0"), R("b0"), 0.0, A.add, A.subtract)
        scan(R("cnt", 416, 832), R("a1"), R("b1"), 0.0, A.add, A.subtract)
        ts(R("cum", 0, 832, 2), R("cnt", 0, 416), R("base", 0, 1), A.add)
        ts(R("cum", 1, 832, 2), R("cnt", 416, 832), R("base", 1, 2), A.add)
        key(0, 192)
        if first:
            fill(R("ymin", 0, 3 * 392, 392), HUGE)
            act(R("crow", 0, 32), R("vrow", 0, 32), F.Identity, bias=-UP * MID, scale=64 * UP)
            act(R("crow", 32, 64), R("vrow", 0, 32), F.Identity, bias=-UP * (MID + 8192), scale=64 * UP)
            act(col(CNL), pw(WLO), F.Copy, scale=0.5)
        turn(R("zt", 0, 416), R("cum", 0, 416))
        turn(R("zt", 416, 832), R("cum", 416, 832))
        scan(R("zs", 0, 416), R("r32"), R("zt", 0, 416), 0.0, A.max, A.min)
        scan(R("zs", 416, 832), R("r32"), R("zt", 416, 832), 0.0, A.max, A.min)
        key(192, C)
        if first:
            act(col(CD), col(CG), F.Identity, bias=1.0, scale=1.0 / 2048 - 1)
            act(col(CU), col(CG), F.Identity, bias=1.0, scale=2047.0)
            act(col(CN), col(CG), F.Identity, bias=1.0, scale=-1.0)
            act(col(CF), pw(WF), F.Identity, bias=col(CNL), scale=-18.0)
            act(col(CP), col(CD), F.Copy, scale=1536.0)
        act(R("him", 0, C), R("key"), F.Relu, bias=MISS - MID, scale=-1.0 / UP)
        act(R("him", C, ASK), R("key", 0, 16), F.Relu, bias=MISS - MID, scale=-1.0 / UP)
        if first:
            act(R("fm", 512, 1024, 4), R("ident"), F.Copy)
            for lo in (0, 768):
                act(R("em", lo, lo + 768), R("junk"), F.Copy, scale=0.0)
            act(R("r16"), R("k16"), F.Sign)
            for b in range(1, 4):
                act(R("em", 512 * (b - 1) + b, 512 * b, 4), R("ident"), F.Copy)
            act(R("dgs"), R("k16"), F.Abs, bias=col(CI), scale=-1.0)
            act(R("m32"), R("r16"), F.Copy)
            act(R("diag"), R("dgs"), F.Relu, bias=1.0, scale=-1.0)
            act(col(CK), col(CD), F.Copy, scale=512.0)
            act(R("hb"), R("hrow"), F.Identity, scale=col(CD))
            fill(R("m32", 16, C, 32), col(CN))
            fill(R("k512"), col(CK))
            fill(R("dist", 34, 288, 36), 4096.0)
            fill(R("dist", 35, 288, 36), 4096.0)
            fill(R("dwin", 0, 4 * 392, 392), 0.0)
        ts(R("lpos", 0, 26), R("zs", 31, 832, 32), 1406.0, A.add, 0.5, A.mult)
        part(0)
        copy((R("srt"), R("lpos", 0, 24)), R("key"))
        part(128)
        scan(R("ymin", 1, 385), R("srt"), R("srt"), HUGE, A.min, A.min)
        part(256)
        lowest(0, 32)
        scan(R("ymin", 393, 777), R("srt"), R("ymin", 0, 384), HUGE, A.min, A.max)
        spread(0, 32)
        lowest(1, 128)
        scan(R("ymin", 785, 1169), R("srt"), R("ymin", 392, 776), HUGE, A.min, A.max)
        spread(1, 128)
        above(0, 32)
        lowest(2, 192)
        above(1, 128)
        below(1, 128)
        below(0, 32)
        spread(2, 192)
        ts(R("r2"), R("firsts", 127, 161), -4096.0 * UP, A.add)
        tt(R("r1"), R("firsts", 128, 162), R("firsts", 31, 65), A.max)
        below(2, 192)
        tt(R("r4"), R("r2"), R("firsts", 30, 64), A.min)
        if first:
            ts(R("fm", 0, 512, 4), R("grow"), col(CGI), A.is_equal, col(CF), A.mult)
        tt(R("r3"), R("r1"), R("firsts", 192, 226), A.min)
        if first:
            quant("eq", "es", "fm", 512, 640, 0)
            mm(4, "eq", "es", 4, "bq", "bs")
        else:
            ask(0, 128)
        tt(R("vi"), R("r3"), R("r4"), A.min)
        if first:
            quant("eq", "es", "fm", 0, 128, 128)
        else:
            ask(128, 256)
        ts(R("vf"), R("vi"), 0x7E003800, A.bitwise_and)
        ts(R("vn"), R("vi"), 14, A.logical_shift_right, 511, A.bitwise_and)
        if first:
            ts(R("tint", 5, 6), p0, 15, A.bitwise_and, 1, A.logical_shift_right)
            ts(R("tint", 6, 7), R("pint", 2, 3), 16, A.bitwise_and)
        else:
            ask(256, C)
        tt(R("tab%d" % t), R("vf"), R("vn"), A.add)
        send("land%d" % t, "tab%d" % t, "gott%d" % t)
        send(npl, pp, "gotp%d" % t)
        if first:
            ask(0, C)
            copy(R("col", CH, CH + 2), R("tint", 5, 7))
            memset(R("fj", 24, 32), 0)
        scan(R("dgs"), R("r16"), R("dg"), 0.0, A.mult, A.add)
        if first:
            act(col(CB2), col(CG), F.Identity, bias=0.75, scale=-1.0 / 16)
            act(col(CB3), col(CL), F.Abs, bias=-16.0)
            act(col(CT), col(CX), F.Identity, bias=col(CH), scale=col(CB2))
            act(col(CZ), col(CB3), F.Relu, bias=12.0, scale=-12.0)
            quant("eq", "es", "em", 128, 256, 0)
        else:
            quant("vq", "vs", "vt")
        ts(R("cap"), R("him"), col(CP), A.min)
        ts(R("lask", 0, 24), R("dgs", 15, C, 16), 143.5, A.add)
        ts(R("lask", 24, 25), R("dgs", 15, 16), 143.5, A.add)
        for h in range(1, 8):
            act(R("dist", 36 * h, 36 * h + 34), R("land%d" % t), F.Abs, bias=R("hb", h, h + 1), scale=col(CD))
            if h == 4:
                ts(R("dist", 0, 34), R("land%d" % t), 1.0, A.add, col(CD), A.mult)
                if first:
                    quant("eq", "es", "em", 256, 384, 128)
                scan(R("ans", 0, 180), R("k512", 0, 180), R("dist", 0, 180), 4096.0, A.add, A.min)
        scan(R("ans", 180, 288), R("k512", 180, 288), R("dist", 180, 288), 4096.0, A.add, A.min)
        if first:
            quant("eq", "es", "em", 384, 512, 256)
        for b in range(4):
            mm(b, "eq", "es", b, nq, npl)
        cut = s1[0]
        tt(R("z2", 0, cut), (R("ans"), R("lask", 0, cut // 16)), R("cap", 0, cut), A.min)
        act(R("zg", cut, ASK), (R("ans"), R("lask", cut // 16, ASK // 16)), F.Copy)
        for b in range(4):
            act(R("dwin", 392 * b + 1, 392 * b + 385), bank(b), F.Copy)
        tt(R("z2", cut, ASK), R("zg", cut, ASK), R("cap", cut, ASK), A.min)
        pieces = ((0, 0, cut), (C, 16, cut - 32), (cut, cut, C - cut), (C + cut - 32, cut - 16, C + 32 - cut))
        for at, lo, w in pieces:
            turn(R("zt2", at, at + w), R("z2", lo, lo + w))
        for at, lo, w in pieces:
            scan(R("zs2", at, at + w), R("m32", 0, w), R("zt2", at, at + w), 0.0, A.mult, A.max)
        if first:
            ts(R("lq", 0, 1), col(CT), col(CZ), A.add)
            ts(R("lq", 1, 2), col(CT), 8.0, A.add)
        ts(R("fi"), R("zs2", 31, 2 * C, 32), col(CU), A.mult)
        ts(R("fj", 0, 24), R("fi"), 511, A.bitwise_and)
        copy(R("lfound"), (R("fj"), R("lq")))
        nx = "x%d" % (t + 1)
        mid = cut + 64
        for lo, hi, bs in ((0, cut, (2, 3)), (mid, C, (0,)), (cut, C, (1, 2, 3))):
            for b in bs:
                act(R("mg", C * b + lo, C * b + hi), found(b, lo, hi), F.Copy)
        for lo, hi, bs, own in ((0, cut, (0, 1), 1), (0, cut, (2, 3), 0), (cut, mid, (0,), 1), (mid, C, (0,), 0), (cut, C, (1, 2, 3), 0)):
            if lo == mid:
                quant("xq%d" % (t + 1), "xs%d" % (t + 1), nx, *s0)
            for b in bs:
                src = found(b, lo, hi) if own else R("mg", C * b + lo, C * b + hi)
                tt(R(nx, 4 * lo + b, 4 * hi, 4), src, R(p, 4 * lo + b, 4 * hi, 4), A.add)

    x, xq, xs = "x%d" % ROUNDS, "xq%d" % ROUNDS, "xs%d" % ROUNDS
    outs = [("out", k, k + 1, 1) for k in range(8)]
    for k, (lo, hi) in enumerate(SPANS):
        if k:
            quant(xq, xs, x, lo, hi)
        mm(5 + k, "vq", "vs", 0, xq, xs, lo, hi)
        dma("s", lambda lo=lo, hi=hi: T.oc[:, 4 * lo:4 * hi], lambda lo=lo, hi=hi: T[xq][:, lo:hi].bitcast(dt.uint8), [R(xq, lo, hi)], [outs[k]])
        if k:
            for m in range(4):
                dma("sa"[m % 2], lambda m=m: T.osc[4 * m:4 * m + 4, :], lambda m=m: T[xs][32 * m:32 * m + 4, :], [R(xs)], [outs[4 + m]])
        act(R("yb", lo, hi), bank(5 + k, hi - lo), F.Copy)
        dma("a", lambda lo=lo, hi=hi: T.y[:, lo:hi], lambda lo=lo, hi=hi: T.yb[:, lo:hi], [R("yb", lo, hi)], [outs[2 + k]])
    add("g", lambda: g.wait_ge(T.sem.sent, 5 * ROUNDS * lanes_out), outs, [], "end")
    emit(g, T, ops)
